import numpy as np
import ml_dtypes


def mxq(x, axis, fmt="e4m3"):
    dtype, down = {"e4m3": (ml_dtypes.float8_e4m3fn, 7), "e5m2": (ml_dtypes.float8_e5m2, 14)}[fmt]
    v = np.moveaxis(np.asarray(x, np.float32).astype(ml_dtypes.bfloat16).astype(np.float64), axis, -1)
    blocks = v.reshape(v.shape[:-1] + (-1, 32))
    amax = np.abs(blocks).max(-1, keepdims=True)
    byte = np.maximum(np.where(amax > 0, np.frexp(amax)[1] - 1 + 127, 0) - down, 1)
    scale = np.exp2(byte - 127.0)
    codes = (blocks / scale).astype(np.float32).astype(dtype).astype(np.float64)
    return np.moveaxis((codes * scale).reshape(v.shape), -1, axis)


WIDE = False


def mx_kscale(k):
    if not WIDE:
        return np.ones(k)
    levels = np.array([10, -10, 5, -5, 0])
    if k % 512:
        return np.exp2(np.random.permutation(np.resize(levels, k // 32))).repeat(32)
    a = np.empty((k // 512, 16))
    for p in range(k // 512):
        a[p, :8] = np.random.permutation(np.resize(levels, 8))
        for g in range(8):
            far = levels[np.abs(levels - a[p, g]) >= 10]
            a[p, g + 8] = far[np.random.randint(len(far))]
    return np.exp2(a.ravel()).repeat(32)


def f64(x):
    return np.asarray(x).astype(np.float64)


def striped(idx):
    return np.tile(idx.reshape(-1, 16).T, (8, 1)).astype(np.uint16)


def unstriped(offs):
    return offs[:16].T.reshape(-1).astype(np.int64)


E2M1 = np.array([0.0, 0.5, 1.0, 1.5, 2.0, 3.0, 4.0, 6.0, -0.0, -0.5, -1.0, -1.5, -2.0, -3.0, -4.0, -6.0])


def pack_weight(w, fmt):
    k, n = w.shape
    w = f64(np.asarray(w, np.float32).astype(ml_dtypes.bfloat16)).reshape(k // 32, 32, n)
    amax = np.abs(w).max(1)
    if fmt == "e4m3":
        byte = np.frexp(amax)[1] - 1 + 127 - 7
    else:
        mant, ex = np.frexp(amax / 6.0)
        byte = np.where(mant > 0.5, ex, ex - 1) + 127
    byte = np.clip(np.where(amax > 0, byte, 1), 1, 254)
    scaled = (w * np.exp2(127.0 - byte)[:, None, :]).reshape(k, n).astype(np.float32)
    by_word = np.ascontiguousarray(scaled.reshape(k // 512, 128, 4, n).transpose(0, 1, 3, 2))
    if fmt == "e4m3":
        words = by_word.astype(ml_dtypes.float8_e4m3fn).view(np.uint8)
    else:
        c = by_word.astype(ml_dtypes.float4_e2m1fn).view(np.uint8) & 0xF
        words = (c[..., 0::2] | (c[..., 1::2] << 4)).reshape(k // 512, 128, 2 * n)
    return np.ascontiguousarray(words), np.ascontiguousarray(byte.astype(np.uint8).reshape(k // 512, 16, n))


def unpack_weight(words, scales, fmt):
    g, _, n = scales.shape
    words = np.ascontiguousarray(words).reshape(g, 128, n, -1)
    if fmt == "e4m3":
        vals = words.view(ml_dtypes.float8_e4m3fn).astype(np.float64)
    else:
        nib = np.empty((g, 128, n, 4), np.uint8)
        nib[..., 0::2] = words & 0xF
        nib[..., 1::2] = words >> 4
        vals = E2M1[nib]
    vals = vals * np.repeat(np.exp2(scales.astype(np.float64) - 127.0), 8, axis=1)[..., None]
    return vals.transpose(0, 1, 3, 2).reshape(g * 512, n)


def gelu(v):
    return 0.5 * v * (1.0 + np.tanh(np.sqrt(2.0 / np.pi) * (v + 0.044715 * v**3)))


def twice(P):
    return np.random.permutation(np.repeat(np.arange(P), 2))


K, H, T, S, P = 1536, 1024, 4096, 1024, 512

def setup_inputs():
    n = np.random.standard_normal
    s = mx_kscale(K)[:, None]
    u = mx_kscale(H)[:, None]
    d = {}
    d["tab_words"], d["tab_scales"] = pack_weight(n((K, T)) * s, "e4m3")
    d["offs"] = striped(np.random.permutation(T)[:S])
    d["pos1"] = striped(np.random.permutation(S)[:P])
    d["pos2"] = striped(np.random.permutation(S)[:P])
    d["pos3"] = striped(twice(P))
    d["w1"] = (n((K, H)) * 0.54 / K ** 0.5 / s).astype(np.float32)
    d["gain"] = (np.exp(0.3 * n(H)) * u[:, 0]).astype(np.float32)
    d["w2_words"], d["w2_scales"] = pack_weight(n((H, H)) * 2.5 / H ** 0.5 / u, "e2m1")
    d["w3"] = (n((H, H)) * 2.5 / H ** 0.5 / u).astype(np.float32)
    return d

def reference(tab_words, tab_scales, offs, pos1, pos2, pos3, w1, gain, w2_words, w2_scales, w3):
    v = unpack_weight(tab_words, tab_scales, "e4m3")[:, unstriped(offs)]
    a = mxq(f64(w1), 0, "e4m3").T @ v
    h = a * np.cos(a)
    z = f64(gain)[:, None] * np.minimum(h[:, unstriped(pos1)], h[:, unstriped(pos2)])
    zq = mxq(z, 0, "e4m3")
    b = unpack_weight(w2_words, w2_scales, "e2m1").T @ zq
    e = mxq(f64(w3), 0, "e4m3").T @ zq
    y = b * e
    return np.tanh(y[:, unstriped(pos3)] + h)

@@ -1,0 +1,336 @@
+import math
+from contextlib import ExitStack
+
+import concourse.mybir as mybir
+
+K, H, T, S, M = 1536, 1024, 4096, 1024, 512
+FLOPS = 2 * K * H * S + 2 * 2 * H * H * M
+
+F32 = mybir.dt.float32
+BF16 = mybir.dt.bfloat16
+I32 = mybir.dt.int32
+U32 = mybir.dt.uint32
+U16 = mybir.dt.uint16
+U8 = mybir.dt.uint8
+FP8X4 = mybir.dt.float8_e4m3fn_x4
+FP4X4 = mybir.dt.float4_e2m1fn_x4
+ALU = mybir.AluOpType
+ACT = mybir.ActivationFunctionType
+
+P = 128
+BANK = 512
+SLOTS = 8
+TWO_PI = 2.0 * math.pi
+TURN_OFFSET = float(2**20)
+QUARTER = 0
+K_ON_VECTOR = (0,)
+SCALE_ON_VECTOR = (7,)
+Y_WIDTH = S + 16
+
+
+def tile_list_shoe_patch_features_kernel(
+    tc, tab_words, tab_scales, offs, pos1, pos2, pos3, w1, gain, w2_words, w2_scales, w3, out
+):
+    nc = tc.nc
+    with ExitStack() as ctx:
+        held = ctx.enter_context(tc.tile_pool(name="held", bufs=1))
+        big = ctx.enter_context(tc.tile_pool(name="big", bufs=3))
+        raws = ctx.enter_context(tc.tile_pool(name="raws", bufs=5))
+        two = ctx.enter_context(tc.tile_pool(name="two", bufs=2))
+        three = ctx.enter_context(tc.tile_pool(name="three", bufs=3))
+        psum = ctx.enter_context(tc.psum_pool(name="psum", bufs=8))
+
+        warm = held.tile([P, 8], F32, name="warm")
+        warm_out = held.tile([P, 8], F32, name="warm_out")
+        nc.gpsimd.memset(warm[:], 0.0)
+        nc.scalar.activation(warm_out[:], warm[:], ACT.Silu)
+
+        idx = held.tile([P, S // 16], U16, name="idx")
+        p1 = held.tile([P, M // 16], U16, name="p1")
+        p2 = held.tile([P, M // 16], U16, name="p2")
+        p3 = held.tile([P, S // 16], U16, name="p3")
+        nc.sync.dma_start(idx[:], offs)
+
+        tab_s = held.tile([P, T], U8, name="tab_s", align_bytes=64)
+        nc.vector.memset(tab_s[:].bitcast(I32), 0)
+        w2s_raw = held.tile([P, 2, H], U8, name="w2s_raw", align_bytes=64)
+        nc.gpsimd.memset(w2s_raw[:].bitcast(I32), 0)
+        gains = held.tile([P, 2, 4], F32, name="gains")
+
+        v_words = [held.tile([P, S], U32, name="v_words%d" % a, align_bytes=64) for a in range(3)]
+        v_scales = held.tile([P, S], U8, name="v_scales", align_bytes=64)
+
+        def load_table(a):
+            words = big.tile([P, T], U32, name="big", align_bytes=64)
+            nc.sync.dma_start(words[:].bitcast(I32), tab_words[a].rearrange("p t i -> p (t i)").bitcast(I32))
+            return words
+
+        def gather_table(a, words, pieces):
+            n = S // pieces
+            for u in range(pieces):
+                nc.vector.tensor_copy(
+                    v_words[a][:, u * n : (u + 1) * n], words[:].indirect(idx[:, u * n // 16 : (u + 1) * n // 16])
+                )
+
+        def load_w1(a, b):
+            raw = raws.tile([P, 4, BANK], F32, name="raw")
+            rows = w1[512 * a : 512 * (a + 1), BANK * b : BANK * (b + 1)]
+            nc.sync.dma_start(raw[:], rows.rearrange("(p j) c -> p j c", j=4))
+            return raw[:]
+
+        def load_w3(a):
+            raw = big.tile([P, 4, H], F32, name="big", align_bytes=64)
+            nc.sync.dma_start(raw[:], w3[512 * a : 512 * (a + 1), :].rearrange("(p j) c -> p j c", j=4))
+            return raw
+
+        def weave(raw, on_vector):
+            woven = three.tile([P, 4 * BANK], BF16, name="woven", align_bytes=64)
+            dst = woven[:].rearrange("p (t m j) -> p m t j", t=4, j=4)
+            src = raw.rearrange("p j (m t) -> p m t j", t=4)
+            if on_vector:
+                nc.vector.tensor_copy(dst, src)
+            else:
+                nc.scalar.copy(dst, src)
+            return woven
+
+        def quantize(woven, name):
+            codes = held.tile([P, BANK], U32, name=name + "_c", align_bytes=64)
+            scales = held.tile([P, BANK], U8, name=name + "_s", align_bytes=64)
+            nc.vector.quantize_mx(out=codes[:].bitcast(FP8X4), scales=scales[:], in_=woven[:])
+            return codes, scales
+
+        tab0 = load_table(0)
+        for q in range(4):
+            nc.sync.dma_start(
+                tab_s[32 * q : 32 * q + 12, :].bitcast(I32), tab_scales[:, 4 * q : 4 * q + 4, :].bitcast(I32)
+            )
+
+        raw00 = load_w1(0, 0)
+        tab1 = load_table(1)
+        raw10 = load_w1(1, 0)
+        for q in range(4):
+            nc.sync.dma_start(
+                w2s_raw[32 * q : 32 * q + 4, :, :].bitcast(I32),
+                w2_scales[:, 4 * q : 4 * q + 4, :].rearrange("a r c -> r a c").bitcast(I32),
+            )
+        raw20 = load_w1(2, 0)
+        w2_raw = raws.tile([P, 2, 2 * H], U8, name="raw")
+        nc.sync.dma_start(w2_raw[:].bitcast(I32), w2_words.rearrange("a p c -> p a c").bitcast(I32))
+        tab2 = load_table(2)
+        nc.sync.dma_start(p1[:], pos1)
+        nc.sync.dma_start(p2[:], pos2)
+        nc.sync.dma_start(gains[:], gain.rearrange("(b p t) -> p b t", b=2, t=4))
+
+        w2c = held.tile([P, 2, 2 * H], U8, name="w2c", align_bytes=64)
+        w2s = held.tile([P, 2, H], U8, name="w2s", align_bytes=64)
+
+        def deal_w2():
+            nc.vector.tensor_copy(
+                w2c[:].rearrange("p a c -> p (a c)").bitcast(U16).rearrange("p (g t u i) -> p g u t i", g=4, t=4, i=8),
+                w2_raw[:].rearrange("p a c -> p (a c)").bitcast(U16).rearrange("p (g u i t) -> p g u t i", g=4, t=4, i=8),
+            )
+            nc.vector.tensor_copy(
+                w2s[:].rearrange("p a (b t u i) -> p (a b) u t i", b=2, t=4, i=16),
+                w2s_raw[:].rearrange("p a (b u i t) -> p (a b) u t i", b=2, t=4, i=16),
+            )
+
+        w1q = {}
+        gather_table(0, tab0, 1)
+        nc.vector.tensor_copy(v_scales[:], tab_s[:].indirect(idx[:]))
+        w1q[0, 0] = quantize(weave(raw00, False), "w1_00")
+        gather_table(1, tab1, 1)
+        w1q[1, 0] = quantize(weave(raw10, False), "w1_10")
+        w1q[2, 0] = quantize(weave(raw20, False), "w1_20")
+        deal_w2()
+        gather_table(2, tab2, 2)
+
+        raw1 = [load_w1(a, 1) for a in range(3)]
+        nc.sync.dma_start(p3[:], pos3)
+
+        raw3 = [load_w3(a) for a in range(2)]
+
+        ys = [held.tile([P, Y_WIDTH], F32, name="y%d" % i) for i in range(2)]
+        for y in ys:
+            nc.gpsimd.memset(y[:, M:], 0.0)
+
+        hs = [held.tile([P, S], F32, name="h%d" % s) for s in range(SLOTS)]
+        accs, args, mins = {}, {}, {}
+        zb, zq, w3q = {}, {}, {}
+
+        def first_product(s, passes=(0, 1, 2)):
+            b, t = divmod(s, 4)
+            cols = slice(P * t, P * (t + 1))
+            if passes[0] == 0:
+                accs[s] = [psum.tile([P, BANK], F32, name="acc") for u in range(2)]
+            for u in range(2):
+                acc = accs[s][u]
+                js = slice(BANK * u, BANK * (u + 1))
+                for a in passes:
+                    codes, scales = w1q[a, b]
+                    nc.tensor.matmul_mx(
+                        out=acc[:], lhsT=codes[:, cols].bitcast(FP8X4), lhsT_scale=scales[:, cols],
+                        rhs=v_words[a][:, js].bitcast(FP8X4), rhs_scale=v_scales[4 * a : P, js],
+                        start=(a == 0), stop=(a == 2),
+                    )
+
+        def turns(s):
+            arg = three.tile([P, S], F32, name="arg")
+            if s in K_ON_VECTOR:
+                k = two.tile([P, S], I32, name="k")
+                for u in range(2):
+                    js = slice(BANK * u, BANK * (u + 1))
+                    nc.vector.tensor_scalar(k[:, js], accs[s][u][:], 1.0 / TWO_PI, QUARTER, ALU.mult, ALU.add)
+                args[s] = (arg, k)
+            else:
+                k = two.tile([P, S], U32, name="k")
+                for u in range(2):
+                    js = slice(BANK * u, BANK * (u + 1))
+                    nc.scalar.activation(k[:, js], accs[s][u][:], ACT.Copy, bias=TURN_OFFSET + QUARTER, scale=1.0 / TWO_PI)
+                nc.scalar.activation(arg[:], k[:], ACT.Copy, bias=TWO_PI * TURN_OFFSET, scale=-TWO_PI)
+                args[s] = (arg, None)
+
+        def reduce_angle(s):
+            arg, k = args[s]
+            for u in range(2):
+                js = slice(BANK * u, BANK * (u + 1))
+                if k is None:
+                    nc.vector.tensor_tensor(arg[:, js], accs[s][u][:], arg[:, js], ALU.add)
+                else:
+                    nc.vector.scalar_tensor_tensor(arg[:, js], k[:, js], -TWO_PI, accs[s][u][:], ALU.mult, ALU.add)
+
+        def cosine(s):
+            arg = args[s][0]
+            n = BANK if s == 0 else S
+            for j0 in range(0, S, n):
+                part = arg[:, j0 : j0 + n]
+                nc.scalar.activation(part, part, ACT.Abs)
+                nc.scalar.activation(part, part, ACT.Sin, bias=math.pi / 2, scale=-1.0)
+
+        def features(s):
+            arg = args[s][0]
+            for u in range(2):
+                js = slice(BANK * u, BANK * (u + 1))
+                nc.vector.tensor_tensor(hs[s][:, js], accs[s][u][:], arg[:, js], ALU.mult)
+
+        def sections(s):
+            b, t = divmod(s, 4)
+            g1 = three.tile([P, M], F32, name="g1")
+            g2 = two.tile([P, M], F32, name="g2")
+            nc.vector.tensor_copy(g1[:], hs[s][:].indirect(p1[:]))
+            nc.vector.tensor_copy(g2[:], hs[s][:].indirect(p2[:]))
+            nc.vector.tensor_tensor(g1[:], g1[:], g2[:], ALU.min)
+            mins[s] = g1
+
+        def scale_section(s):
+            b, t = divmod(s, 4)
+            if t == 0:
+                zb[b] = two.tile([P, 4, M], BF16, name="zb", align_bytes=64)
+            if s in SCALE_ON_VECTOR:
+                nc.vector.tensor_scalar(zb[b][:, t, :], mins[s][:], gains[:, b, t : t + 1], None, ALU.mult)
+            else:
+                nc.scalar.activation(zb[b][:, t, :], mins[s][:], ACT.Copy, scale=gains[:, b, t : t + 1])
+
+        def quantize_z(b):
+            woven = three.tile([P, 4 * M], BF16, name="woven", align_bytes=64)
+            nc.vector.tensor_copy(
+                woven[:].rearrange("p (c i t) -> p c t i", i=4, t=4), zb[b][:].rearrange("p t (c i) -> p c t i", i=4)
+            )
+            zq[b] = quantize(woven, "z%d" % b)
+
+        pending = {}
+
+        def weave_job(job):
+            if job[0] == "w1":
+                pending[job] = weave(raw1[job[1]], False)
+            else:
+                pending[job] = weave(raw3[job[1]][:, :, BANK * job[2] : BANK * (job[2] + 1)], False)
+
+        def quantize_job(job):
+            if job[0] == "w1":
+                w1q[job[1], 1] = quantize(pending[job], "w1_%d1" % job[1])
+            else:
+                w3q[job[1], job[2]] = quantize(pending[job], "w3_%d%d" % (job[1], job[2]))
+
+        jobs = {0: [("w1", 0), ("w1", 1)], 1: [("w1", 2)], 3: [("w3", 0, 0)], 5: [("w3", 1, 0)], 7: [("w3", 0, 1), ("w3", 1, 1)]}
+
+        first_product(0, (0, 1))
+        first_product(1, (0, 1))
+        first_product(0, (2,))
+        first_product(1, (2,))
+        turns(0)
+        reduce_angle(0)
+        turns(1)
+        cosine(0)
+        for s in range(SLOTS):
+            if s + 2 < SLOTS:
+                first_product(s + 2)
+                turns(s + 2)
+            if s + 1 < SLOTS:
+                reduce_angle(s + 1)
+            features(s)
+            if s + 1 < SLOTS:
+                cosine(s + 1)
+            if s >= 1:
+                scale_section(s - 1)
+            for job in jobs.get(s, []):
+                weave_job(job)
+            sections(s)
+            if s == 4:
+                quantize_z(0)
+            if s < SLOTS - 1:
+                for job in jobs.get(s, []):
+                    quantize_job(job)
+        scale_section(SLOTS - 1)
+        quantize_z(1)
+        for job in jobs.get(SLOTS - 1, []):
+            quantize_job(job)
+
+        prods = {}
+
+        def second_products(s):
+            b, t = divmod(s, 4)
+            cols = slice(P * t, P * (t + 1))
+            n0 = BANK * b + P * t
+            acc_b = psum.tile([P, M], F32, name="acc")
+            acc_e = psum.tile([P, M], F32, name="acc")
+            for a in range(2):
+                nc.tensor.matmul_mx(
+                    out=acc_b[:], lhsT=w2c[:, a, 2 * n0 : 2 * (n0 + P)].bitcast(FP4X4), lhsT_scale=w2s[:, a, n0 : n0 + P],
+                    rhs=zq[a][0][:].bitcast(FP8X4), rhs_scale=zq[a][1][:], start=(a == 0), stop=(a == 1),
+                )
+            for a in range(2):
+                codes, scales = w3q[a, b]
+                nc.tensor.matmul_mx(
+                    out=acc_e[:], lhsT=codes[:, cols].bitcast(FP8X4), lhsT_scale=scales[:, cols],
+                    rhs=zq[a][0][:].bitcast(FP8X4), rhs_scale=zq[a][1][:], start=(a == 0), stop=(a == 1),
+                )
+            b_sb = three.tile([P, M], F32, name="g1")
+            nc.scalar.copy(b_sb[:], acc_b[:])
+            prods[s] = (b_sb, acc_e)
+
+        def multiply(s):
+            b_sb, acc_e = prods[s]
+            nc.vector.tensor_tensor(ys[s % 2][:, :M], acc_e[:], b_sb[:], ALU.mult)
+
+        def finish(s):
+            b, t = divmod(s, 4)
+            cuts = (0, 512, 768, S) if s == SLOTS - 1 else (0, S)
+            rows = out[BANK * b : BANK * (b + 1), :].rearrange("(p t) j -> p t j", t=4)
+            for j0, j1 in zip(cuts, cuts[1:]):
+                js = slice(j0, j1)
+                total = three.tile([P, j1 - j0], F32, name="arg")
+                nc.vector.tensor_tensor(
+                    total[:], ys[s % 2][:].indirect(p3[:, j0 // 16 : j1 // 16]), hs[s][:, js], ALU.add
+                )
+                nc.scalar.activation(total[:], total[:], ACT.Tanh)
+                nc.sync.dma_start(rows[:, t, js], total[:])
+
+        second_products(0)
+        second_products(1)
+        multiply(0)
+        for s in range(SLOTS):
+            if s + 2 < SLOTS:
+                second_products(s + 2)
+            if s + 1 < SLOTS:
+                multiply(s + 1)
+            finish(s)

@@ -25,6 +25,8 @@ TURN_OFFSET = float(2**20)
 QUARTER = 0
 K_ON_VECTOR = (0,)
 SCALE_ON_VECTOR = (7,)
+WEAVE_ON_VECTOR = (("w1", 0),("w1", 1),)
+Z_ON_SCALAR = ()
 Y_WIDTH = S + 16
 
 
@@ -83,9 +85,10 @@ def tile_list_shoe_patch_features_kernel(
             nc.sync.dma_start(raw[:], w3[512 * a : 512 * (a + 1), :].rearrange("(p j) c -> p j c", j=4))
             return raw
 
-        def weave(raw, on_vector):
-            woven = three.tile([P, 4 * BANK], BF16, name="woven", align_bytes=64)
-            dst = woven[:].rearrange("p (t m j) -> p m t j", t=4, j=4)
+        def weave(raw, on_vector, woven=None):
+            if woven is None:
+                woven = three.tile([P, 4 * BANK], BF16, name="woven", align_bytes=64)[:]
+            dst = woven.rearrange("p (t m j) -> p m t j", t=4, j=4)
             src = raw.rearrange("p j (m t) -> p m t j", t=4)
             if on_vector:
                 nc.vector.tensor_copy(dst, src)
@@ -96,10 +99,29 @@ def tile_list_shoe_patch_features_kernel(
         def quantize(woven, name):
             codes = held.tile([P, BANK], U32, name=name + "_c", align_bytes=64)
             scales = held.tile([P, BANK], U8, name=name + "_s", align_bytes=64)
-            nc.vector.quantize_mx(out=codes[:].bitcast(FP8X4), scales=scales[:], in_=woven[:])
+            nc.vector.quantize_mx(out=codes[:].bitcast(FP8X4), scales=scales[:], in_=woven)
+            return codes, scales
+
+        def weave_and_quantize_by_slot(raw, name):
+            woven = three.tile([P, 4 * BANK], BF16, name="woven", align_bytes=64)
+            codes = held.tile([P, BANK], U32, name=name + "_c", align_bytes=64)
+            scales = held.tile([P, BANK], U8, name=name + "_s", align_bytes=64)
+            dst = woven[:].rearrange("p (t m j) -> p m t j", t=4, j=4)
+            src = raw.rearrange("p j (m t) -> p m t j", t=4)
+            nc.vector.tensor_copy(dst[:, :, 0:2, :], src[:, :, 0:2, :])
+            nc.scalar.copy(dst[:, :, 2:4, :], src[:, :, 2:4, :])
+            for h in range(2):
+                cols = slice(2 * P * h, 2 * P * (h + 1))
+                nc.vector.quantize_mx(
+                    out=codes[:, cols].bitcast(FP8X4), scales=scales[:, cols], in_=woven[:, 8 * P * h : 8 * P * (h + 1)]
+                )
             return codes, scales
 
         tab0 = load_table(0)
+        nc.sync.dma_start(p1[:], pos1)
+        nc.sync.dma_start(p2[:], pos2)
+        nc.sync.dma_start(gains[:], gain.rearrange("(b p t) -> p b t", b=2, t=4))
+        nc.sync.dma_start(p3[:], pos3)
         for q in range(4):
             nc.sync.dma_start(
                 tab_s[32 * q : 32 * q + 12, :].bitcast(I32), tab_scales[:, 4 * q : 4 * q + 4, :].bitcast(I32)
@@ -107,19 +129,16 @@ def tile_list_shoe_patch_features_kernel(
 
         raw00 = load_w1(0, 0)
         tab1 = load_table(1)
+        tab2 = load_table(2)
         raw10 = load_w1(1, 0)
         for q in range(4):
             nc.sync.dma_start(
                 w2s_raw[32 * q : 32 * q + 4, :, :].bitcast(I32),
                 w2_scales[:, 4 * q : 4 * q + 4, :].rearrange("a r c -> r a c").bitcast(I32),
             )
-        raw20 = load_w1(2, 0)
-        w2_raw = raws.tile([P, 2, 2 * H], U8, name="raw")
+        w2_raw = held.tile([P, 2, 2 * H], U8, name="w2_raw")
         nc.sync.dma_start(w2_raw[:].bitcast(I32), w2_words.rearrange("a p c -> p a c").bitcast(I32))
-        tab2 = load_table(2)
-        nc.sync.dma_start(p1[:], pos1)
-        nc.sync.dma_start(p2[:], pos2)
-        nc.sync.dma_start(gains[:], gain.rearrange("(b p t) -> p b t", b=2, t=4))
+        raw20 = load_w1(2, 0)
 
         w2c = held.tile([P, 2, 2 * H], U8, name="w2c", align_bytes=64)
         w2s = held.tile([P, 2, H], U8, name="w2s", align_bytes=64)
@@ -136,16 +155,15 @@ def tile_list_shoe_patch_features_kernel(
 
         w1q = {}
         gather_table(0, tab0, 1)
-        nc.vector.tensor_copy(v_scales[:], tab_s[:].indirect(idx[:]))
         w1q[0, 0] = quantize(weave(raw00, False), "w1_00")
         gather_table(1, tab1, 1)
+        nc.vector.tensor_copy(v_scales[:], tab_s[:].indirect(idx[:]))
+        gather_table(2, tab2, 1)
         w1q[1, 0] = quantize(weave(raw10, False), "w1_10")
-        w1q[2, 0] = quantize(weave(raw20, False), "w1_20")
         deal_w2()
-        gather_table(2, tab2, 2)
+        w1q[2, 0] = weave_and_quantize_by_slot(raw20, "w1_20")
 
         raw1 = [load_w1(a, 1) for a in range(3)]
-        nc.sync.dma_start(p3[:], pos3)
 
         raw3 = [load_w3(a) for a in range(2)]
 
@@ -154,8 +172,9 @@ def tile_list_shoe_patch_features_kernel(
             nc.gpsimd.memset(y[:, M:], 0.0)
 
         hs = [held.tile([P, S], F32, name="h%d" % s) for s in range(SLOTS)]
-        accs, args, mins = {}, {}, {}
-        zb, zq, w3q = {}, {}, {}
+        accs, args, mins, picks = {}, {}, {}, {}
+        zb = held.tile([P, 4, M], BF16, name="zb", align_bytes=64)
+        zq, w3q = {}, {}
 
         def first_product(s, passes=(0, 1, 2)):
             b, t = divmod(s, 4)
@@ -174,15 +193,15 @@ def tile_list_shoe_patch_features_kernel(
                     )
 
         def turns(s):
-            arg = three.tile([P, S], F32, name="arg")
+            arg = three.tile([P, S], F32, name="arg", bufs=4)
             if s in K_ON_VECTOR:
-                k = two.tile([P, S], I32, name="k")
+                k = two.tile([P, S], I32, name="k", align_bytes=64)
                 for u in range(2):
                     js = slice(BANK * u, BANK * (u + 1))
                     nc.vector.tensor_scalar(k[:, js], accs[s][u][:], 1.0 / TWO_PI, QUARTER, ALU.mult, ALU.add)
                 args[s] = (arg, k)
             else:
-                k = two.tile([P, S], U32, name="k")
+                k = two.tile([P, S], U32, name="k", align_bytes=64)
                 for u in range(2):
                     js = slice(BANK * u, BANK * (u + 1))
                     nc.scalar.activation(k[:, js], accs[s][u][:], ACT.Copy, bias=TURN_OFFSET + QUARTER, scale=1.0 / TWO_PI)
@@ -214,36 +233,38 @@ def tile_list_shoe_patch_features_kernel(
 
         def sections(s):
             b, t = divmod(s, 4)
-            g1 = three.tile([P, M], F32, name="g1")
+            g1 = two.tile([P, M], F32, name="g1")
             g2 = two.tile([P, M], F32, name="g2")
             nc.vector.tensor_copy(g1[:], hs[s][:].indirect(p1[:]))
             nc.vector.tensor_copy(g2[:], hs[s][:].indirect(p2[:]))
-            nc.vector.tensor_tensor(g1[:], g1[:], g2[:], ALU.min)
-            mins[s] = g1
+            picks[s] = (g1, g2)
+
+        def smaller(s):
+            g1, g2 = picks[s]
+            mins[s] = args[min(s + 1, SLOTS - 1)][0][:, (M if s == SLOTS - 1 else 0) : (S if s == SLOTS - 1 else M)]
+            nc.vector.tensor_tensor(mins[s], g1[:], g2[:], ALU.min)
 
         def scale_section(s):
             b, t = divmod(s, 4)
-            if t == 0:
-                zb[b] = two.tile([P, 4, M], BF16, name="zb", align_bytes=64)
             if s in SCALE_ON_VECTOR:
-                nc.vector.tensor_scalar(zb[b][:, t, :], mins[s][:], gains[:, b, t : t + 1], None, ALU.mult)
+                nc.vector.tensor_scalar(zb[:, t, :], mins[s], gains[:, b, t : t + 1], None, ALU.mult)
             else:
-                nc.scalar.activation(zb[b][:, t, :], mins[s][:], ACT.Copy, scale=gains[:, b, t : t + 1])
+                nc.scalar.activation(zb[:, t, :], mins[s], ACT.Copy, scale=gains[:, b, t : t + 1])
 
         def quantize_z(b):
-            woven = three.tile([P, 4 * M], BF16, name="woven", align_bytes=64)
-            nc.vector.tensor_copy(
-                woven[:].rearrange("p (c i t) -> p c t i", i=4, t=4), zb[b][:].rearrange("p t (c i) -> p c t i", i=4)
-            )
-            zq[b] = quantize(woven, "z%d" % b)
+            woven = two.tile([P, 4 * M], BF16, name="k", align_bytes=64)
+            copy = nc.scalar.copy if b in Z_ON_SCALAR else nc.vector.tensor_copy
+            copy(woven[:].rearrange("p (c i t) -> p c t i", i=4, t=4), zb[:].rearrange("p t (c i) -> p c t i", i=4))
+            zq[b] = quantize(woven[:], "z%d" % b)
 
         pending = {}
 
         def weave_job(job):
             if job[0] == "w1":
-                pending[job] = weave(raw1[job[1]], False)
+                pending[job] = weave(raw1[job[1]], job in WEAVE_ON_VECTOR)
             else:
-                pending[job] = weave(raw3[job[1]][:, :, BANK * job[2] : BANK * (job[2] + 1)], False)
+                pending[job] = weave(raw3[job[1]][:, :, BANK * job[2] : BANK * (job[2] + 1)], job in WEAVE_ON_VECTOR,
+                                     zb[:].rearrange("p t m -> p (t m)") if job == ("w3", 1, 1) else None)
 
         def quantize_job(job):
             if job[0] == "w1":
@@ -251,14 +272,18 @@ def tile_list_shoe_patch_features_kernel(
             else:
                 w3q[job[1], job[2]] = quantize(pending[job], "w3_%d%d" % (job[1], job[2]))
 
-        jobs = {0: [("w1", 0), ("w1", 1)], 1: [("w1", 2)], 3: [("w3", 0, 0)], 5: [("w3", 1, 0)], 7: [("w3", 0, 1), ("w3", 1, 1)]}
+        jobs = {-1: [("w1", 0), ("w1", 1)], 0: [("w1", 2)], 7: [("w3", 0, 0), ("w3", 1, 0), ("w3", 0, 1)], 8: [("w3", 1, 1)]}
 
         first_product(0, (0, 1))
         first_product(1, (0, 1))
         first_product(0, (2,))
         first_product(1, (2,))
+        for job in jobs.get(-1, []):
+            weave_job(job)
         turns(0)
         reduce_angle(0)
+        for job in jobs.get(-1, []):
+            quantize_job(job)
         turns(1)
         cosine(0)
         for s in range(SLOTS):
@@ -271,6 +296,7 @@ def tile_list_shoe_patch_features_kernel(
             if s + 1 < SLOTS:
                 cosine(s + 1)
             if s >= 1:
+                smaller(s - 1)
                 scale_section(s - 1)
             for job in jobs.get(s, []):
                 weave_job(job)
@@ -280,10 +306,11 @@ def tile_list_shoe_patch_features_kernel(
             if s < SLOTS - 1:
                 for job in jobs.get(s, []):
                     quantize_job(job)
-        scale_section(SLOTS - 1)
-        quantize_z(1)
         for job in jobs.get(SLOTS - 1, []):
             quantize_job(job)
+        smaller(SLOTS - 1)
+        scale_section(SLOTS - 1)
+        quantize_z(1)
 
         prods = {}
 
@@ -304,13 +331,16 @@ def tile_list_shoe_patch_features_kernel(
                     out=acc_e[:], lhsT=codes[:, cols].bitcast(FP8X4), lhsT_scale=scales[:, cols],
                     rhs=zq[a][0][:].bitcast(FP8X4), rhs_scale=zq[a][1][:], start=(a == 0), stop=(a == 1),
                 )
-            b_sb = three.tile([P, M], F32, name="g1")
-            nc.scalar.copy(b_sb[:], acc_b[:])
+            if s == 0:
+                b_sb = zb[:].rearrange("p t m -> p (t m)").bitcast(F32)[:, :M]
+            else:
+                b_sb = two.tile([P, M], F32, name="g1" if s % 2 else "g2")[:]
+            nc.scalar.copy(b_sb, acc_b[:])
             prods[s] = (b_sb, acc_e)
 
         def multiply(s):
             b_sb, acc_e = prods[s]
-            nc.vector.tensor_tensor(ys[s % 2][:, :M], acc_e[:], b_sb[:], ALU.mult)
+            nc.vector.tensor_tensor(ys[s % 2][:, :M], acc_e[:], b_sb, ALU.mult)
 
         def finish(s):
             b, t = divmod(s, 4)
@@ -318,7 +348,7 @@ def tile_list_shoe_patch_features_kernel(
             rows = out[BANK * b : BANK * (b + 1), :].rearrange("(p t) j -> p t j", t=4)
             for j0, j1 in zip(cuts, cuts[1:]):
                 js = slice(j0, j1)
-                total = three.tile([P, j1 - j0], F32, name="arg")
+                total = raws.tile([P, j1 - j0], F32, name="raw")
                 nc.vector.tensor_tensor(
                     total[:], ys[s % 2][:].indirect(p3[:, j0 // 16 : j1 // 16]), hs[s][:, js], ALU.add
                 )
@@ -333,4 +363,8 @@ def tile_list_shoe_patch_features_kernel(
                 second_products(s + 2)
             if s + 1 < SLOTS:
                 multiply(s + 1)
+            for job in jobs.get(SLOTS + s, []):
+                weave_job(job)
             finish(s)
+            for job in jobs.get(SLOTS + s, []):
+                quantize_job(job)

@@ -27,6 +27,7 @@ K_ON_VECTOR = (0,)
 SCALE_ON_VECTOR = (7,)
 WEAVE_ON_VECTOR = (("w1", 0),("w1", 1),)
 Z_ON_SCALAR = ()
+H_ON_VECTOR = (0,)
 Y_WIDTH = S + 16
 
 
@@ -192,30 +193,28 @@ def tile_list_shoe_patch_features_kernel(
                         start=(a == 0), stop=(a == 2),
                     )
 
-        def turns(s):
-            arg = three.tile([P, S], F32, name="arg", bufs=4)
-            if s in K_ON_VECTOR:
-                k = two.tile([P, S], I32, name="k", align_bytes=64)
-                for u in range(2):
-                    js = slice(BANK * u, BANK * (u + 1))
-                    nc.vector.tensor_scalar(k[:, js], accs[s][u][:], 1.0 / TWO_PI, QUARTER, ALU.mult, ALU.add)
-                args[s] = (arg, k)
-            else:
-                k = two.tile([P, S], U32, name="k", align_bytes=64)
-                for u in range(2):
-                    js = slice(BANK * u, BANK * (u + 1))
-                    nc.scalar.activation(k[:, js], accs[s][u][:], ACT.Copy, bias=TURN_OFFSET + QUARTER, scale=1.0 / TWO_PI)
-                nc.scalar.activation(arg[:], k[:], ACT.Copy, bias=TWO_PI * TURN_OFFSET, scale=-TWO_PI)
-                args[s] = (arg, None)
+        ring = [held.tile([P, S], F32, name="arg%d" % i, align_bytes=64) for i in range(3)]
+        copies = {}
 
-        def reduce_angle(s):
-            arg, k = args[s]
+        def turns(s):
+            arg = ring[s % 3]
+            args[s] = (arg,)
+            if s not in H_ON_VECTOR:
+                copies[s] = three.tile([P, S], F32, name="a_sb", bufs=4)
             for u in range(2):
                 js = slice(BANK * u, BANK * (u + 1))
-                if k is None:
-                    nc.vector.tensor_tensor(arg[:, js], accs[s][u][:], arg[:, js], ALU.add)
-                else:
-                    nc.vector.scalar_tensor_tensor(arg[:, js], k[:, js], -TWO_PI, accs[s][u][:], ALU.mult, ALU.add)
+                if s in K_ON_VECTOR:
+                    nc.vector.tensor_scalar(arg[:, js].bitcast(I32), accs[s][u][:], 1.0 / TWO_PI, 0.0, ALU.mult, ALU.add)
+                if s not in H_ON_VECTOR:
+                    nc.scalar.copy(copies[s][:, js], accs[s][u][:])
+            if s not in K_ON_VECTOR:
+                nc.gpsimd.tensor_scalar(arg[:].bitcast(I32), copies[s][:], 1.0 / TWO_PI, 0.0, ALU.mult, ALU.add)
+
+        def reduce_angle(s):
+            arg = args[s][0]
+            for u in range(2):
+                js = slice(BANK * u, BANK * (u + 1))
+                nc.vector.scalar_tensor_tensor(arg[:, js], arg[:, js].bitcast(I32), -TWO_PI, accs[s][u][:], ALU.mult, ALU.add)
 
         def cosine(s):
             arg = args[s][0]
@@ -229,20 +228,23 @@ def tile_list_shoe_patch_features_kernel(
             arg = args[s][0]
             for u in range(2):
                 js = slice(BANK * u, BANK * (u + 1))
-                nc.vector.tensor_tensor(hs[s][:, js], accs[s][u][:], arg[:, js], ALU.mult)
+                if s in H_ON_VECTOR:
+                    nc.vector.tensor_tensor(hs[s][:, js], accs[s][u][:], arg[:, js], ALU.mult)
+                else:
+                    nc.gpsimd.tensor_tensor(hs[s][:, js], copies[s][:, js], arg[:, js], ALU.mult)
 
         def sections(s):
             b, t = divmod(s, 4)
-            g1 = two.tile([P, M], F32, name="g1")
-            g2 = two.tile([P, M], F32, name="g2")
-            nc.vector.tensor_copy(g1[:], hs[s][:].indirect(p1[:]))
-            nc.vector.tensor_copy(g2[:], hs[s][:].indirect(p2[:]))
+            pair = hs[s + 2] if s + 2 < SLOTS else three.tile([P, S], F32, name="a_sb", bufs=4)
+            g1, g2 = pair[:, :M], pair[:, M:]
+            nc.vector.tensor_copy(g1, hs[s][:].indirect(p1[:]))
+            nc.vector.tensor_copy(g2, hs[s][:].indirect(p2[:]))
             picks[s] = (g1, g2)
 
         def smaller(s):
             g1, g2 = picks[s]
-            mins[s] = args[min(s + 1, SLOTS - 1)][0][:, (M if s == SLOTS - 1 else 0) : (S if s == SLOTS - 1 else M)]
-            nc.vector.tensor_tensor(mins[s], g1[:], g2[:], ALU.min)
+            mins[s] = two.tile([P, M], F32, name="g1")[:]
+            nc.vector.tensor_tensor(mins[s], g1, g2, ALU.min)
 
         def scale_section(s):
             b, t = divmod(s, 4)
@@ -252,7 +254,7 @@ def tile_list_shoe_patch_features_kernel(
                 nc.scalar.activation(zb[:, t, :], mins[s], ACT.Copy, scale=gains[:, b, t : t + 1])
 
         def quantize_z(b):
-            woven = two.tile([P, 4 * M], BF16, name="k", align_bytes=64)
+            woven = three.tile([P, 4 * M], BF16, name="woven", align_bytes=64)
             copy = nc.scalar.copy if b in Z_ON_SCALAR else nc.vector.tensor_copy
             copy(woven[:].rearrange("p (c i t) -> p c t i", i=4, t=4), zb[:].rearrange("p t (c i) -> p c t i", i=4))
             zq[b] = quantize(woven[:], "z%d" % b)
@@ -272,31 +274,39 @@ def tile_list_shoe_patch_features_kernel(
             else:
                 w3q[job[1], job[2]] = quantize(pending[job], "w3_%d%d" % (job[1], job[2]))
 
-        jobs = {-1: [("w1", 0), ("w1", 1)], 0: [("w1", 2)], 7: [("w3", 0, 0), ("w3", 1, 0), ("w3", 0, 1)], 8: [("w3", 1, 1)]}
+        jobs = {-1: [("w1", 0), ("w1", 1), ("w1", 2)], 4: [("w3", 0, 0)], 6: [("w3", 1, 0)], 7: [("w3", 0, 1)], 8: [("w3", 1, 1)]}
 
         first_product(0, (0, 1))
         first_product(1, (0, 1))
         first_product(0, (2,))
         first_product(1, (2,))
-        for job in jobs.get(-1, []):
-            weave_job(job)
         turns(0)
         reduce_angle(0)
+        turns(1)
+        first_product(2)
+        cosine(0)
+        turns(2)
+        reduce_angle(1)
+        first_product(3)
+        features(0)
+        cosine(1)
+        turns(3)
+        for job in jobs.get(-1, []):
+            weave_job(job)
         for job in jobs.get(-1, []):
             quantize_job(job)
-        turns(1)
-        cosine(0)
         for s in range(SLOTS):
-            if s + 2 < SLOTS:
-                first_product(s + 2)
-                turns(s + 2)
-            if s + 1 < SLOTS:
-                reduce_angle(s + 1)
-            features(s)
-            if s + 1 < SLOTS:
-                cosine(s + 1)
             if s >= 1:
                 smaller(s - 1)
+            if s + 1 < SLOTS:
+                features(s + 1)
+            if s + 2 < SLOTS:
+                reduce_angle(s + 2)
+                cosine(s + 2)
+            if s + 4 < SLOTS:
+                first_product(s + 4)
+                turns(s + 4)
+            if s >= 1:
                 scale_section(s - 1)
             for job in jobs.get(s, []):
                 weave_job(job)
@@ -334,7 +344,7 @@ def tile_list_shoe_patch_features_kernel(
             if s == 0:
                 b_sb = zb[:].rearrange("p t m -> p (t m)").bitcast(F32)[:, :M]
             else:
-                b_sb = two.tile([P, M], F32, name="g1" if s % 2 else "g2")[:]
+                b_sb = two.tile([P, M], F32, name="g1")[:]
             nc.scalar.copy(b_sb, acc_b[:])
             prods[s] = (b_sb, acc_e)
 

@@ -26,8 +26,10 @@ QUARTER = 0
 K_ON_VECTOR = (0,)
 SCALE_ON_VECTOR = (7,)
 WEAVE_ON_VECTOR = (("w1", 0),("w1", 1),)
-Z_ON_SCALAR = ()
+Z_ON_SCALAR = (0,)
 H_ON_VECTOR = (0,)
+K_SPLIT = 256
+WEAVE_ON_GPSIMD = ()
 Y_WIDTH = S + 16
 
 
@@ -41,7 +43,7 @@ def tile_list_shoe_patch_features_kernel(
         raws = ctx.enter_context(tc.tile_pool(name="raws", bufs=5))
         two = ctx.enter_context(tc.tile_pool(name="two", bufs=2))
         three = ctx.enter_context(tc.tile_pool(name="three", bufs=3))
-        psum = ctx.enter_context(tc.psum_pool(name="psum", bufs=8))
+        psum = ctx.enter_context(tc.psum_pool(name="psum", bufs=4))
 
         warm = held.tile([P, 8], F32, name="warm")
         warm_out = held.tile([P, 8], F32, name="warm_out")
@@ -91,7 +93,9 @@ def tile_list_shoe_patch_features_kernel(
                 woven = three.tile([P, 4 * BANK], BF16, name="woven", align_bytes=64)[:]
             dst = woven.rearrange("p (t m j) -> p m t j", t=4, j=4)
             src = raw.rearrange("p j (m t) -> p m t j", t=4)
-            if on_vector:
+            if on_vector == "gpsimd":
+                nc.gpsimd.tensor_scalar(dst, src, 1.0, 0.0, ALU.mult, ALU.add)
+            elif on_vector:
                 nc.vector.tensor_copy(dst, src)
             else:
                 nc.scalar.copy(dst, src)
@@ -123,22 +127,22 @@ def tile_list_shoe_patch_features_kernel(
         nc.sync.dma_start(p2[:], pos2)
         nc.sync.dma_start(gains[:], gain.rearrange("(b p t) -> p b t", b=2, t=4))
         nc.sync.dma_start(p3[:], pos3)
+        raw00 = load_w1(0, 0)
+        w2_raw = held.tile([P, 2, 2 * H], U8, name="w2_raw")
+        nc.sync.dma_start(w2_raw[:].bitcast(I32), w2_words.rearrange("a p c -> p a c").bitcast(I32))
         for q in range(4):
             nc.sync.dma_start(
                 tab_s[32 * q : 32 * q + 12, :].bitcast(I32), tab_scales[:, 4 * q : 4 * q + 4, :].bitcast(I32)
             )
 
-        raw00 = load_w1(0, 0)
         tab1 = load_table(1)
-        tab2 = load_table(2)
-        raw10 = load_w1(1, 0)
         for q in range(4):
             nc.sync.dma_start(
                 w2s_raw[32 * q : 32 * q + 4, :, :].bitcast(I32),
                 w2_scales[:, 4 * q : 4 * q + 4, :].rearrange("a r c -> r a c").bitcast(I32),
             )
-        w2_raw = held.tile([P, 2, 2 * H], U8, name="w2_raw")
-        nc.sync.dma_start(w2_raw[:].bitcast(I32), w2_words.rearrange("a p c -> p a c").bitcast(I32))
+        raw10 = load_w1(1, 0)
+        tab2 = load_table(2)
         raw20 = load_w1(2, 0)
 
         w2c = held.tile([P, 2, 2 * H], U8, name="w2c", align_bytes=64)
@@ -156,12 +160,12 @@ def tile_list_shoe_patch_features_kernel(
 
         w1q = {}
         gather_table(0, tab0, 1)
+        nc.vector.tensor_copy(v_scales[:], tab_s[:].indirect(idx[:]))
         w1q[0, 0] = quantize(weave(raw00, False), "w1_00")
         gather_table(1, tab1, 1)
-        nc.vector.tensor_copy(v_scales[:], tab_s[:].indirect(idx[:]))
-        gather_table(2, tab2, 1)
-        w1q[1, 0] = quantize(weave(raw10, False), "w1_10")
         deal_w2()
+        w1q[1, 0] = quantize(weave(raw10, False), "w1_10")
+        gather_table(2, tab2, 1)
         w1q[2, 0] = weave_and_quantize_by_slot(raw20, "w1_20")
 
         raw1 = [load_w1(a, 1) for a in range(3)]
@@ -181,7 +185,7 @@ def tile_list_shoe_patch_features_kernel(
             b, t = divmod(s, 4)
             cols = slice(P * t, P * (t + 1))
             if passes[0] == 0:
-                accs[s] = [psum.tile([P, BANK], F32, name="acc") for u in range(2)]
+                accs[s] = [psum.tile([P, BANK], F32, name="acc%d" % u) for u in range(2)]
             for u in range(2):
                 acc = accs[s][u]
                 js = slice(BANK * u, BANK * (u + 1))
@@ -208,7 +212,9 @@ def tile_list_shoe_patch_features_kernel(
                 if s not in H_ON_VECTOR:
                     nc.scalar.copy(copies[s][:, js], accs[s][u][:])
             if s not in K_ON_VECTOR:
-                nc.gpsimd.tensor_scalar(arg[:].bitcast(I32), copies[s][:], 1.0 / TWO_PI, 0.0, ALU.mult, ALU.add)
+                if K_SPLIT:
+                    nc.vector.tensor_scalar(arg[:, :K_SPLIT].bitcast(I32), accs[s][0][:, :K_SPLIT], 1.0 / TWO_PI, 0.0, ALU.mult, ALU.add)
+                nc.gpsimd.tensor_scalar(arg[:, K_SPLIT:].bitcast(I32), copies[s][:, K_SPLIT:], 1.0 / TWO_PI, 0.0, ALU.mult, ALU.add)
 
         def reduce_angle(s):
             arg = args[s][0]
@@ -221,8 +227,9 @@ def tile_list_shoe_patch_features_kernel(
             n = BANK if s == 0 else S
             for j0 in range(0, S, n):
                 part = arg[:, j0 : j0 + n]
-                nc.scalar.activation(part, part, ACT.Abs)
-                nc.scalar.activation(part, part, ACT.Sin, bias=math.pi / 2, scale=-1.0)
+                folded = ring[2][:] if s == SLOTS - 1 else part
+                nc.scalar.activation(folded, part, ACT.Abs)
+                nc.scalar.activation(part, folded, ACT.Sin, bias=math.pi / 2, scale=-1.0)
 
         def features(s):
             arg = args[s][0]
@@ -243,7 +250,7 @@ def tile_list_shoe_patch_features_kernel(
 
         def smaller(s):
             g1, g2 = picks[s]
-            mins[s] = two.tile([P, M], F32, name="g1")[:]
+            mins[s] = three.tile([P, M], F32, name="g1")[:]
             nc.vector.tensor_tensor(mins[s], g1, g2, ALU.min)
 
         def scale_section(s):
@@ -260,13 +267,19 @@ def tile_list_shoe_patch_features_kernel(
             zq[b] = quantize(woven[:], "z%d" % b)
 
         pending = {}
+        w3_homes = {
+            (0, 0): ring[2][:].bitcast(BF16),
+            (1, 0): ring[0][:].bitcast(BF16),
+            (0, 1): ring[1][:].bitcast(BF16),
+            (1, 1): zb[:].rearrange("p t m -> p (t m)"),
+        }
 
         def weave_job(job):
             if job[0] == "w1":
-                pending[job] = weave(raw1[job[1]], job in WEAVE_ON_VECTOR)
+                pending[job] = weave(raw1[job[1]], "gpsimd" if job in WEAVE_ON_GPSIMD else job in WEAVE_ON_VECTOR)
             else:
                 pending[job] = weave(raw3[job[1]][:, :, BANK * job[2] : BANK * (job[2] + 1)], job in WEAVE_ON_VECTOR,
-                                     zb[:].rearrange("p t m -> p (t m)") if job == ("w3", 1, 1) else None)
+                                     w3_homes[job[1], job[2]])
 
         def quantize_job(job):
             if job[0] == "w1":
@@ -274,7 +287,7 @@ def tile_list_shoe_patch_features_kernel(
             else:
                 w3q[job[1], job[2]] = quantize(pending[job], "w3_%d%d" % (job[1], job[2]))
 
-        jobs = {-1: [("w1", 0), ("w1", 1), ("w1", 2)], 4: [("w3", 0, 0)], 6: [("w3", 1, 0)], 7: [("w3", 0, 1)], 8: [("w3", 1, 1)]}
+        jobs = {-1: [("w1", 0), ("w1", 1), ("w1", 2)], 6: [("w3", 0, 0), ("w3", 1, 0)], 7: [("w3", 0, 1)], 8: [("w3", 1, 1)]}
 
         first_product(0, (0, 1))
         first_product(1, (0, 1))
@@ -328,8 +341,8 @@ def tile_list_shoe_patch_features_kernel(
             b, t = divmod(s, 4)
             cols = slice(P * t, P * (t + 1))
             n0 = BANK * b + P * t
-            acc_b = psum.tile([P, M], F32, name="acc")
-            acc_e = psum.tile([P, M], F32, name="acc")
+            acc_b = psum.tile([P, M], F32, name="acc0")
+            acc_e = psum.tile([P, M], F32, name="acc1")
             for a in range(2):
                 nc.tensor.matmul_mx(
                     out=acc_b[:], lhsT=w2c[:, a, 2 * n0 : 2 * (n0 + P)].bitcast(FP4X4), lhsT_scale=w2s[:, a, n0 : n0 + P],
@@ -344,7 +357,7 @@ def tile_list_shoe_patch_features_kernel(
             if s == 0:
                 b_sb = zb[:].rearrange("p t m -> p (t m)").bitcast(F32)[:, :M]
             else:
-                b_sb = two.tile([P, M], F32, name="g1")[:]
+                b_sb = three.tile([P, M], F32, name="g1")[:]
             nc.scalar.copy(b_sb, acc_b[:])
             prods[s] = (b_sb, acc_e)
 

@@ -18,19 +18,15 @@ ALU = mybir.AluOpType
 ACT = mybir.ActivationFunctionType
 
 P = 128
+PACK = 4
+K_PASS = P * PACK
 BANK = 512
-SLOTS = 8
+SLOTS = H // P
+LAST = SLOTS - 1
 TWO_PI = 2.0 * math.pi
-TURN_OFFSET = float(2**20)
-QUARTER = 0
-K_ON_VECTOR = (0,)
-SCALE_ON_VECTOR = (7,)
-WEAVE_ON_VECTOR = (("w1", 0),("w1", 1),)
-Z_ON_SCALAR = (0,)
-H_ON_VECTOR = (0,)
-K_SPLIT = 256
-WEAVE_ON_GPSIMD = ()
+TURNS_ON_VECTOR = 256
 Y_WIDTH = S + 16
+LAST_CUTS = (0, 512, 768, S)
 
 
 def tile_list_shoe_patch_features_kernel(
@@ -41,14 +37,12 @@ def tile_list_shoe_patch_features_kernel(
         held = ctx.enter_context(tc.tile_pool(name="held", bufs=1))
         big = ctx.enter_context(tc.tile_pool(name="big", bufs=3))
         raws = ctx.enter_context(tc.tile_pool(name="raws", bufs=5))
-        two = ctx.enter_context(tc.tile_pool(name="two", bufs=2))
         three = ctx.enter_context(tc.tile_pool(name="three", bufs=3))
         psum = ctx.enter_context(tc.psum_pool(name="psum", bufs=4))
 
-        warm = held.tile([P, 8], F32, name="warm")
-        warm_out = held.tile([P, 8], F32, name="warm_out")
-        nc.gpsimd.memset(warm[:], 0.0)
-        nc.scalar.activation(warm_out[:], warm[:], ACT.Silu)
+        ys = [held.tile([P, Y_WIDTH], F32, name="y%d" % i) for i in range(3)]
+        nc.gpsimd.memset(ys[0][:, M:S], 0.0)
+        nc.scalar.activation(ys[0][:, S:], ys[0][:, M : M + Y_WIDTH - S], ACT.Silu)
 
         idx = held.tile([P, S // 16], U16, name="idx")
         p1 = held.tile([P, M // 16], U16, name="p1")
@@ -60,254 +54,232 @@ def tile_list_shoe_patch_features_kernel(
         nc.vector.memset(tab_s[:].bitcast(I32), 0)
         w2s_raw = held.tile([P, 2, H], U8, name="w2s_raw", align_bytes=64)
         nc.gpsimd.memset(w2s_raw[:].bitcast(I32), 0)
-        gains = held.tile([P, 2, 4], F32, name="gains")
+        gains = held.tile([P, 2, PACK], F32, name="gains")
 
-        v_words = [held.tile([P, S], U32, name="v_words%d" % a, align_bytes=64) for a in range(3)]
+        v_words = [held.tile([P, S], U32, name="v_words%d" % g, align_bytes=64) for g in range(3)]
         v_scales = held.tile([P, S], U8, name="v_scales", align_bytes=64)
 
-        def load_table(a):
+        def load_table(g, pieces=1):
             words = big.tile([P, T], U32, name="big", align_bytes=64)
-            nc.sync.dma_start(words[:].bitcast(I32), tab_words[a].rearrange("p t i -> p (t i)").bitcast(I32))
+            rows = tab_words[g].rearrange("p t i -> p (t i)").bitcast(I32)
+            width = T // pieces
+            for c0 in range(0, T, width):
+                nc.sync.dma_start(words[:, c0 : c0 + width].bitcast(I32), rows[:, c0 : c0 + width])
             return words
 
-        def gather_table(a, words, pieces):
-            n = S // pieces
-            for u in range(pieces):
-                nc.vector.tensor_copy(
-                    v_words[a][:, u * n : (u + 1) * n], words[:].indirect(idx[:, u * n // 16 : (u + 1) * n // 16])
-                )
+        def gather_table(g, words):
+            nc.vector.tensor_copy(v_words[g][:], words[:].indirect(idx[:]))
 
-        def load_w1(a, b):
-            raw = raws.tile([P, 4, BANK], F32, name="raw")
-            rows = w1[512 * a : 512 * (a + 1), BANK * b : BANK * (b + 1)]
-            nc.sync.dma_start(raw[:], rows.rearrange("(p j) c -> p j c", j=4))
+        def load_w1(g, b, pieces=1):
+            raw = raws.tile([P, PACK, K_PASS], F32, name="raw")
+            rows = w1[K_PASS * g : K_PASS * (g + 1), K_PASS * b : K_PASS * (b + 1)]
+            rows = rows.rearrange("(p i) c -> p i c", i=PACK)
+            depth = PACK // pieces
+            for i0 in range(0, PACK, depth):
+                nc.sync.dma_start(raw[:, i0 : i0 + depth, :], rows[:, i0 : i0 + depth, :])
             return raw[:]
 
-        def load_w3(a):
-            raw = big.tile([P, 4, H], F32, name="big", align_bytes=64)
-            nc.sync.dma_start(raw[:], w3[512 * a : 512 * (a + 1), :].rearrange("(p j) c -> p j c", j=4))
+        def load_w3(g):
+            raw = big.tile([P, PACK, H], F32, name="big", align_bytes=64)
+            nc.sync.dma_start(raw[:], w3[K_PASS * g : K_PASS * (g + 1), :].rearrange("(p i) c -> p i c", i=PACK))
             return raw
 
-        def weave(raw, on_vector, woven=None):
-            if woven is None:
-                woven = three.tile([P, 4 * BANK], BF16, name="woven", align_bytes=64)[:]
-            dst = woven.rearrange("p (t m j) -> p m t j", t=4, j=4)
-            src = raw.rearrange("p j (m t) -> p m t j", t=4)
-            if on_vector == "gpsimd":
-                nc.gpsimd.tensor_scalar(dst, src, 1.0, 0.0, ALU.mult, ALU.add)
-            elif on_vector:
-                nc.vector.tensor_copy(dst, src)
-            else:
-                nc.scalar.copy(dst, src)
+        def new_woven():
+            return three.tile([P, PACK * K_PASS], BF16, name="woven", align_bytes=64)[:]
+
+        def weave(copy, woven, raw, t0=0, slots=PACK):
+            dealt = raw.rearrange("p i (m t) -> p m t i", t=PACK)[:, :, t0 : t0 + slots, :]
+            copy(woven.rearrange("p (t m i) -> p m t i", t=slots, i=PACK), dealt)
             return woven
 
-        def quantize(woven, name):
-            codes = held.tile([P, BANK], U32, name=name + "_c", align_bytes=64)
-            scales = held.tile([P, BANK], U8, name=name + "_s", align_bytes=64)
-            nc.vector.quantize_mx(out=codes[:].bitcast(FP8X4), scales=scales[:], in_=woven)
+        def quantize(name, *parts):
+            codes = held.tile([P, K_PASS], U32, name=name + "_codes", align_bytes=64)
+            scales = held.tile([P, K_PASS], U8, name=name + "_scales", align_bytes=64)
+            width = K_PASS // len(parts)
+            for i, part in enumerate(parts):
+                cols = slice(width * i, width * (i + 1))
+                nc.vector.quantize_mx(out=codes[:, cols].bitcast(FP8X4), scales=scales[:, cols], in_=part)
             return codes, scales
 
-        def weave_and_quantize_by_slot(raw, name):
-            woven = three.tile([P, 4 * BANK], BF16, name="woven", align_bytes=64)
-            codes = held.tile([P, BANK], U32, name=name + "_c", align_bytes=64)
-            scales = held.tile([P, BANK], U8, name=name + "_s", align_bytes=64)
-            dst = woven[:].rearrange("p (t m j) -> p m t j", t=4, j=4)
-            src = raw.rearrange("p j (m t) -> p m t j", t=4)
-            nc.vector.tensor_copy(dst[:, :, 0:2, :], src[:, :, 0:2, :])
-            nc.scalar.copy(dst[:, :, 2:4, :], src[:, :, 2:4, :])
-            for h in range(2):
-                cols = slice(2 * P * h, 2 * P * (h + 1))
-                nc.vector.quantize_mx(
-                    out=codes[:, cols].bitcast(FP8X4), scales=scales[:, cols], in_=woven[:, 8 * P * h : 8 * P * (h + 1)]
-                )
-            return codes, scales
-
-        tab0 = load_table(0)
-        nc.sync.dma_start(p1[:], pos1)
-        nc.sync.dma_start(p2[:], pos2)
-        nc.sync.dma_start(gains[:], gain.rearrange("(b p t) -> p b t", b=2, t=4))
-        nc.sync.dma_start(p3[:], pos3)
-        raw00 = load_w1(0, 0)
-        w2_raw = held.tile([P, 2, 2 * H], U8, name="w2_raw")
-        nc.sync.dma_start(w2_raw[:].bitcast(I32), w2_words.rearrange("a p c -> p a c").bitcast(I32))
+        tab0 = load_table(0, pieces=4)
+        raw00 = load_w1(0, 0, pieces=2)
+        w2_raw = three.tile([P, 2, 2 * H], U8, name="woven", align_bytes=64)
+        nc.sync.dma_start(w2_raw[:].bitcast(I32), w2_words.rearrange("g p c -> p g c").bitcast(I32))
         for q in range(4):
             nc.sync.dma_start(
                 tab_s[32 * q : 32 * q + 12, :].bitcast(I32), tab_scales[:, 4 * q : 4 * q + 4, :].bitcast(I32)
             )
-
         tab1 = load_table(1)
         for q in range(4):
             nc.sync.dma_start(
                 w2s_raw[32 * q : 32 * q + 4, :, :].bitcast(I32),
-                w2_scales[:, 4 * q : 4 * q + 4, :].rearrange("a r c -> r a c").bitcast(I32),
+                w2_scales[:, 4 * q : 4 * q + 4, :].rearrange("g r c -> r g c").bitcast(I32),
             )
         raw10 = load_w1(1, 0)
         tab2 = load_table(2)
         raw20 = load_w1(2, 0)
 
-        w2c = held.tile([P, 2, 2 * H], U8, name="w2c", align_bytes=64)
-        w2s = held.tile([P, 2, H], U8, name="w2s", align_bytes=64)
+        w2_codes = held.tile([P, 2, 2 * H], U8, name="w2_codes", align_bytes=64)
+        w2_dealt_scales = held.tile([P, 2, H], U8, name="w2_dealt_scales", align_bytes=64)
 
         def deal_w2():
+            words_out = w2_codes[:].rearrange("p g c -> p (g c)").bitcast(U16)
+            words_in = w2_raw[:].rearrange("p g c -> p (g c)").bitcast(U16)
             nc.vector.tensor_copy(
-                w2c[:].rearrange("p a c -> p (a c)").bitcast(U16).rearrange("p (g t u i) -> p g u t i", g=4, t=4, i=8),
-                w2_raw[:].rearrange("p a c -> p (a c)").bitcast(U16).rearrange("p (g u i t) -> p g u t i", g=4, t=4, i=8),
+                words_out.rearrange("p (e t u v) -> p e u t v", e=4, t=PACK, v=8),
+                words_in.rearrange("p (e u v t) -> p e u t v", e=4, t=PACK, v=8),
             )
             nc.vector.tensor_copy(
-                w2s[:].rearrange("p a (b t u i) -> p (a b) u t i", b=2, t=4, i=16),
-                w2s_raw[:].rearrange("p a (b u i t) -> p (a b) u t i", b=2, t=4, i=16),
+                w2_dealt_scales[:].rearrange("p g (b t u v) -> p (g b) u t v", b=2, t=PACK, v=16),
+                w2s_raw[:].rearrange("p g (b u v t) -> p (g b) u t v", b=2, t=PACK, v=16),
             )
 
         w1q = {}
-        gather_table(0, tab0, 1)
+        gather_table(0, tab0)
         nc.vector.tensor_copy(v_scales[:], tab_s[:].indirect(idx[:]))
-        w1q[0, 0] = quantize(weave(raw00, False), "w1_00")
-        gather_table(1, tab1, 1)
+        w1q[0, 0] = quantize("w1_00", weave(nc.scalar.copy, new_woven(), raw00))
+        gather_table(1, tab1)
         deal_w2()
-        w1q[1, 0] = quantize(weave(raw10, False), "w1_10")
-        gather_table(2, tab2, 1)
-        w1q[2, 0] = weave_and_quantize_by_slot(raw20, "w1_20")
+        w1q[1, 0] = quantize("w1_10", weave(nc.scalar.copy, new_woven(), raw10))
+        gather_table(2, tab2)
+        woven = new_woven()
+        first_two, last_two = woven[:, : 2 * K_PASS], woven[:, 2 * K_PASS :]
+        weave(nc.vector.tensor_copy, first_two, raw20, t0=0, slots=2)
+        weave(nc.scalar.copy, last_two, raw20, t0=2, slots=2)
+        w1q[2, 0] = quantize("w1_20", first_two, last_two)
 
-        raw1 = [load_w1(a, 1) for a in range(3)]
-
-        raw3 = [load_w3(a) for a in range(2)]
-
-        ys = [held.tile([P, Y_WIDTH], F32, name="y%d" % i) for i in range(2)]
-        for y in ys:
+        raw1 = [load_w1(g, 1) for g in range(3)]
+        nc.sync.dma_start(p1[:], pos1)
+        nc.sync.dma_start(p2[:], pos2)
+        nc.sync.dma_start(gains[:], gain.rearrange("(b p t) -> p b t", b=2, t=PACK))
+        nc.sync.dma_start(p3[:], pos3)
+        raw3 = [load_w3(g) for g in range(2)]
+        for y in ys[1:]:
             nc.gpsimd.memset(y[:, M:], 0.0)
 
-        hs = [held.tile([P, S], F32, name="h%d" % s) for s in range(SLOTS)]
-        accs, args, mins, picks = {}, {}, {}, {}
-        zb = held.tile([P, 4, M], BF16, name="zb", align_bytes=64)
-        zq, w3q = {}, {}
+        hs = [held.tile([P, S], F32, name="h%d" % s, align_bytes=64) for s in range(SLOTS)]
+        angles = [held.tile([P, S], F32, name="angle%d" % i, align_bytes=64) for i in range(3)]
+        z_rows = held.tile([P, PACK, M], BF16, name="z_rows", align_bytes=64)
+        z_bytes = z_rows[:].rearrange("p t m -> p (t m)")
+        accs, a_copies, pairs, smallest, zq, w3q, w3_woven = {}, {}, {}, {}, {}, {}, {}
+        halves = [slice(0, BANK), slice(BANK, S)]
+
+        def new_a_tile():
+            return three.tile([P, S], F32, name="a_copy", bufs=4)
 
         def first_product(s, passes=(0, 1, 2)):
-            b, t = divmod(s, 4)
+            b, t = divmod(s, PACK)
             cols = slice(P * t, P * (t + 1))
             if passes[0] == 0:
                 accs[s] = [psum.tile([P, BANK], F32, name="acc%d" % u) for u in range(2)]
-            for u in range(2):
-                acc = accs[s][u]
-                js = slice(BANK * u, BANK * (u + 1))
-                for a in passes:
-                    codes, scales = w1q[a, b]
+            for acc, js in zip(accs[s], halves):
+                for g in passes:
+                    codes, scales = w1q[g, b]
                     nc.tensor.matmul_mx(
                         out=acc[:], lhsT=codes[:, cols].bitcast(FP8X4), lhsT_scale=scales[:, cols],
-                        rhs=v_words[a][:, js].bitcast(FP8X4), rhs_scale=v_scales[4 * a : P, js],
-                        start=(a == 0), stop=(a == 2),
+                        rhs=v_words[g][:, js].bitcast(FP8X4), rhs_scale=v_scales[4 * g : P, js],
+                        start=(g == 0), stop=(g == 2),
                     )
 
-        ring = [held.tile([P, S], F32, name="arg%d" % i, align_bytes=64) for i in range(3)]
-        copies = {}
+        def count_turns(engine, turns, a):
+            engine.tensor_scalar(turns.bitcast(I32), a, 1.0 / TWO_PI, 0.0, ALU.mult, ALU.add)
 
-        def turns(s):
-            arg = ring[s % 3]
-            args[s] = (arg,)
-            if s not in H_ON_VECTOR:
-                copies[s] = three.tile([P, S], F32, name="a_sb", bufs=4)
-            for u in range(2):
-                js = slice(BANK * u, BANK * (u + 1))
-                if s in K_ON_VECTOR:
-                    nc.vector.tensor_scalar(arg[:, js].bitcast(I32), accs[s][u][:], 1.0 / TWO_PI, 0.0, ALU.mult, ALU.add)
-                if s not in H_ON_VECTOR:
-                    nc.scalar.copy(copies[s][:, js], accs[s][u][:])
-            if s not in K_ON_VECTOR:
-                if K_SPLIT:
-                    nc.vector.tensor_scalar(arg[:, :K_SPLIT].bitcast(I32), accs[s][0][:, :K_SPLIT], 1.0 / TWO_PI, 0.0, ALU.mult, ALU.add)
-                nc.gpsimd.tensor_scalar(arg[:, K_SPLIT:].bitcast(I32), copies[s][:, K_SPLIT:], 1.0 / TWO_PI, 0.0, ALU.mult, ALU.add)
+        def turns_of(s):
+            angle = angles[s % 3]
+            if s == 0:
+                for acc, js in zip(accs[s], halves):
+                    count_turns(nc.vector, angle[:, js], acc[:])
+                return
+            a_copies[s] = new_a_tile()
+            for acc, js in zip(accs[s], halves):
+                nc.scalar.copy(a_copies[s][:, js], acc[:])
+            count_turns(nc.vector, angle[:, :TURNS_ON_VECTOR], accs[s][0][:, :TURNS_ON_VECTOR])
+            count_turns(nc.gpsimd, angle[:, TURNS_ON_VECTOR:], a_copies[s][:, TURNS_ON_VECTOR:])
 
         def reduce_angle(s):
-            arg = args[s][0]
-            for u in range(2):
-                js = slice(BANK * u, BANK * (u + 1))
-                nc.vector.scalar_tensor_tensor(arg[:, js], arg[:, js].bitcast(I32), -TWO_PI, accs[s][u][:], ALU.mult, ALU.add)
+            angle = angles[s % 3]
+            for acc, js in zip(accs[s], halves):
+                nc.vector.scalar_tensor_tensor(
+                    angle[:, js], angle[:, js].bitcast(I32), -TWO_PI, acc[:], ALU.mult, ALU.add
+                )
 
         def cosine(s):
-            arg = args[s][0]
-            n = BANK if s == 0 else S
-            for j0 in range(0, S, n):
-                part = arg[:, j0 : j0 + n]
-                folded = ring[2][:] if s == SLOTS - 1 else part
+            for js in halves if s == 0 else [slice(0, S)]:
+                part = angles[s % 3][:, js]
+                folded = angles[2][:] if s == LAST else part
                 nc.scalar.activation(folded, part, ACT.Abs)
                 nc.scalar.activation(part, folded, ACT.Sin, bias=math.pi / 2, scale=-1.0)
 
         def features(s):
-            arg = args[s][0]
-            for u in range(2):
-                js = slice(BANK * u, BANK * (u + 1))
-                if s in H_ON_VECTOR:
-                    nc.vector.tensor_tensor(hs[s][:, js], accs[s][u][:], arg[:, js], ALU.mult)
+            for u, js in enumerate(halves):
+                if s == 0:
+                    nc.vector.tensor_tensor(hs[s][:, js], accs[s][u][:], angles[0][:, js], ALU.mult)
                 else:
-                    nc.gpsimd.tensor_tensor(hs[s][:, js], copies[s][:, js], arg[:, js], ALU.mult)
+                    nc.gpsimd.tensor_tensor(hs[s][:, js], a_copies[s][:, js], angles[s % 3][:, js], ALU.mult)
 
-        def sections(s):
-            b, t = divmod(s, 4)
-            pair = hs[s + 2] if s + 2 < SLOTS else three.tile([P, S], F32, name="a_sb", bufs=4)
-            g1, g2 = pair[:, :M], pair[:, M:]
-            nc.vector.tensor_copy(g1, hs[s][:].indirect(p1[:]))
-            nc.vector.tensor_copy(g2, hs[s][:].indirect(p2[:]))
-            picks[s] = (g1, g2)
+        def pick_pairs(s):
+            pairs[s] = hs[s + 2] if s + 2 < SLOTS else new_a_tile()
+            nc.vector.tensor_copy(pairs[s][:, :M], hs[s][:].indirect(p1[:]))
+            nc.vector.tensor_copy(pairs[s][:, M:], hs[s][:].indirect(p2[:]))
+
+        def new_row():
+            return three.tile([P, M], F32, name="row")[:]
 
         def smaller(s):
-            g1, g2 = picks[s]
-            mins[s] = three.tile([P, M], F32, name="g1")[:]
-            nc.vector.tensor_tensor(mins[s], g1, g2, ALU.min)
+            smallest[s] = new_row()
+            nc.vector.tensor_tensor(smallest[s], pairs[s][:, :M], pairs[s][:, M:], ALU.min)
 
-        def scale_section(s):
-            b, t = divmod(s, 4)
-            if s in SCALE_ON_VECTOR:
-                nc.vector.tensor_scalar(zb[:, t, :], mins[s], gains[:, b, t : t + 1], None, ALU.mult)
+        def apply_gain(s):
+            b, t = divmod(s, PACK)
+            if s == LAST:
+                nc.vector.tensor_scalar(z_rows[:, t, :], smallest[s], gains[:, b, t : t + 1], None, ALU.mult)
             else:
-                nc.scalar.activation(zb[:, t, :], mins[s], ACT.Copy, scale=gains[:, b, t : t + 1])
+                nc.scalar.activation(z_rows[:, t, :], smallest[s], ACT.Copy, scale=gains[:, b, t : t + 1])
 
-        def quantize_z(b):
-            woven = three.tile([P, 4 * M], BF16, name="woven", align_bytes=64)
-            copy = nc.scalar.copy if b in Z_ON_SCALAR else nc.vector.tensor_copy
-            copy(woven[:].rearrange("p (c i t) -> p c t i", i=4, t=4), zb[:].rearrange("p t (c i) -> p c t i", i=4))
-            zq[b] = quantize(woven[:], "z%d" % b)
+        def quantize_z(b, copy):
+            z_woven = new_woven()
+            copy(
+                z_woven.rearrange("p (c v t) -> p c t v", v=4, t=PACK),
+                z_rows[:].rearrange("p t (c v) -> p c t v", v=4),
+            )
+            zq[b] = quantize("z%d" % b, z_woven)
 
-        pending = {}
         w3_homes = {
-            (0, 0): ring[2][:].bitcast(BF16),
-            (1, 0): ring[0][:].bitcast(BF16),
-            (0, 1): ring[1][:].bitcast(BF16),
-            (1, 1): zb[:].rearrange("p t m -> p (t m)"),
+            (0, 0): angles[2][:].bitcast(BF16),
+            (1, 0): angles[0][:].bitcast(BF16),
+            (0, 1): angles[1][:].bitcast(BF16),
+            (1, 1): z_bytes,
         }
 
-        def weave_job(job):
-            if job[0] == "w1":
-                pending[job] = weave(raw1[job[1]], "gpsimd" if job in WEAVE_ON_GPSIMD else job in WEAVE_ON_VECTOR)
-            else:
-                pending[job] = weave(raw3[job[1]][:, :, BANK * job[2] : BANK * (job[2] + 1)], job in WEAVE_ON_VECTOR,
-                                     w3_homes[job[1], job[2]])
+        def weave_w3(g, b):
+            w3_woven[g, b] = weave(nc.scalar.copy, w3_homes[g, b], raw3[g][:, :, K_PASS * b : K_PASS * (b + 1)])
 
-        def quantize_job(job):
-            if job[0] == "w1":
-                w1q[job[1], 1] = quantize(pending[job], "w1_%d1" % job[1])
-            else:
-                w3q[job[1], job[2]] = quantize(pending[job], "w3_%d%d" % (job[1], job[2]))
-
-        jobs = {-1: [("w1", 0), ("w1", 1), ("w1", 2)], 6: [("w3", 0, 0), ("w3", 1, 0)], 7: [("w3", 0, 1)], 8: [("w3", 1, 1)]}
+        def quantize_w3(g, b):
+            w3q[g, b] = quantize("w3_%d%d" % (g, b), w3_woven[g, b])
 
         first_product(0, (0, 1))
         first_product(1, (0, 1))
         first_product(0, (2,))
         first_product(1, (2,))
-        turns(0)
+        turns_of(0)
         reduce_angle(0)
-        turns(1)
+        w1q[0, 1] = quantize("w1_01", weave(nc.vector.tensor_copy, new_woven(), raw1[0]))
+        turns_of(1)
         first_product(2)
         cosine(0)
-        turns(2)
         reduce_angle(1)
         first_product(3)
-        features(0)
         cosine(1)
-        turns(3)
-        for job in jobs.get(-1, []):
-            weave_job(job)
-        for job in jobs.get(-1, []):
-            quantize_job(job)
+        parts = [home[:, :BANK].bitcast(BF16) for home in (angles[2], hs[0])]
+        for i, part in enumerate(parts):
+            weave(nc.vector.tensor_copy, part, raw1[1], t0=2 * i, slots=2)
+        w1q[1, 1] = quantize("w1_11", *parts)
+        turns_of(2)
+        features(0)
+        turns_of(3)
+        w1q[2, 1] = quantize("w1_21", weave(nc.scalar.copy, new_woven(), raw1[2]))
+
+        w3_steps = {LAST - 1: [(0, 0), (1, 0)], LAST: [(0, 1)]}
         for s in range(SLOTS):
             if s >= 1:
                 smaller(s - 1)
@@ -318,65 +290,59 @@ def tile_list_shoe_patch_features_kernel(
                 cosine(s + 2)
             if s + 4 < SLOTS:
                 first_product(s + 4)
-                turns(s + 4)
+                turns_of(s + 4)
             if s >= 1:
-                scale_section(s - 1)
-            for job in jobs.get(s, []):
-                weave_job(job)
-            sections(s)
-            if s == 4:
-                quantize_z(0)
-            if s < SLOTS - 1:
-                for job in jobs.get(s, []):
-                    quantize_job(job)
-        for job in jobs.get(SLOTS - 1, []):
-            quantize_job(job)
-        smaller(SLOTS - 1)
-        scale_section(SLOTS - 1)
-        quantize_z(1)
+                apply_gain(s - 1)
+            for piece in w3_steps.get(s, []):
+                weave_w3(*piece)
+            pick_pairs(s)
+            if s == PACK:
+                quantize_z(0, nc.scalar.copy)
+            for piece in w3_steps.get(s, []):
+                quantize_w3(*piece)
+        smaller(LAST)
+        apply_gain(LAST)
+        quantize_z(1, nc.vector.tensor_copy)
 
-        prods = {}
+        factors = {}
 
         def second_products(s):
-            b, t = divmod(s, 4)
+            b, t = divmod(s, PACK)
             cols = slice(P * t, P * (t + 1))
-            n0 = BANK * b + P * t
-            acc_b = psum.tile([P, M], F32, name="acc0")
-            acc_e = psum.tile([P, M], F32, name="acc1")
-            for a in range(2):
+            c0 = K_PASS * b + P * t
+            acc_w2 = psum.tile([P, M], F32, name="acc0")
+            acc_w3 = psum.tile([P, M], F32, name="acc1")
+            for g in range(2):
                 nc.tensor.matmul_mx(
-                    out=acc_b[:], lhsT=w2c[:, a, 2 * n0 : 2 * (n0 + P)].bitcast(FP4X4), lhsT_scale=w2s[:, a, n0 : n0 + P],
-                    rhs=zq[a][0][:].bitcast(FP8X4), rhs_scale=zq[a][1][:], start=(a == 0), stop=(a == 1),
+                    out=acc_w2[:], lhsT=w2_codes[:, g, 2 * c0 : 2 * (c0 + P)].bitcast(FP4X4),
+                    lhsT_scale=w2_dealt_scales[:, g, c0 : c0 + P],
+                    rhs=zq[g][0][:].bitcast(FP8X4), rhs_scale=zq[g][1][:], start=(g == 0), stop=(g == 1),
                 )
-            for a in range(2):
-                codes, scales = w3q[a, b]
+            for g in range(2):
+                codes, scales = w3q[g, b]
                 nc.tensor.matmul_mx(
-                    out=acc_e[:], lhsT=codes[:, cols].bitcast(FP8X4), lhsT_scale=scales[:, cols],
-                    rhs=zq[a][0][:].bitcast(FP8X4), rhs_scale=zq[a][1][:], start=(a == 0), stop=(a == 1),
+                    out=acc_w3[:], lhsT=codes[:, cols].bitcast(FP8X4), lhsT_scale=scales[:, cols],
+                    rhs=zq[g][0][:].bitcast(FP8X4), rhs_scale=zq[g][1][:], start=(g == 0), stop=(g == 1),
                 )
-            if s == 0:
-                b_sb = zb[:].rearrange("p t m -> p (t m)").bitcast(F32)[:, :M]
-            else:
-                b_sb = three.tile([P, M], F32, name="g1")[:]
-            nc.scalar.copy(b_sb, acc_b[:])
-            prods[s] = (b_sb, acc_e)
+            factor = z_bytes.bitcast(F32)[:, :M] if s == 0 else new_row()
+            nc.scalar.copy(factor, acc_w2[:])
+            factors[s] = (factor, acc_w3)
 
         def multiply(s):
-            b_sb, acc_e = prods[s]
-            nc.vector.tensor_tensor(ys[s % 2][:, :M], acc_e[:], b_sb, ALU.mult)
+            factor, acc_w3 = factors[s]
+            nc.vector.tensor_tensor(ys[s % 3][:, :M], acc_w3[:], factor, ALU.mult)
 
         def finish(s):
-            b, t = divmod(s, 4)
-            cuts = (0, 512, 768, S) if s == SLOTS - 1 else (0, S)
-            rows = out[BANK * b : BANK * (b + 1), :].rearrange("(p t) j -> p t j", t=4)
+            b, t = divmod(s, PACK)
+            cuts = LAST_CUTS if s == LAST else (0, S)
+            rows = out[K_PASS * b : K_PASS * (b + 1), :].rearrange("(p t) j -> p t j", t=PACK)
             for j0, j1 in zip(cuts, cuts[1:]):
-                js = slice(j0, j1)
                 total = raws.tile([P, j1 - j0], F32, name="raw")
                 nc.vector.tensor_tensor(
-                    total[:], ys[s % 2][:].indirect(p3[:, j0 // 16 : j1 // 16]), hs[s][:, js], ALU.add
+                    total[:], ys[s % 3][:].indirect(p3[:, j0 // 16 : j1 // 16]), hs[s][:, j0:j1], ALU.add
                 )
                 nc.scalar.activation(total[:], total[:], ACT.Tanh)
-                nc.sync.dma_start(rows[:, t, js], total[:])
+                nc.sync.dma_start(rows[:, t, j0:j1], total[:])
 
         second_products(0)
         second_products(1)
@@ -386,8 +352,8 @@ def tile_list_shoe_patch_features_kernel(
                 second_products(s + 2)
             if s + 1 < SLOTS:
                 multiply(s + 1)
-            for job in jobs.get(SLOTS + s, []):
-                weave_job(job)
+            if s == 0:
+                weave_w3(1, 1)
             finish(s)
-            for job in jobs.get(SLOTS + s, []):
-                quantize_job(job)
+            if s == 0:
+                quantize_w3(1, 1)

import math
from contextlib import ExitStack

import concourse.mybir as mybir

K, H, T, S, M = 1536, 1024, 4096, 1024, 512
FLOPS = 2 * K * H * S + 2 * 2 * H * H * M

F32 = mybir.dt.float32
BF16 = mybir.dt.bfloat16
I32 = mybir.dt.int32
U32 = mybir.dt.uint32
U16 = mybir.dt.uint16
U8 = mybir.dt.uint8
FP8X4 = mybir.dt.float8_e4m3fn_x4
FP4X4 = mybir.dt.float4_e2m1fn_x4
ALU = mybir.AluOpType
ACT = mybir.ActivationFunctionType

P = 128
PACK = 4
K_PASS = P * PACK
BANK = 512
SLOTS = H // P
LAST = SLOTS - 1
TWO_PI = 2.0 * math.pi
TURNS_ON_VECTOR = 256
Y_WIDTH = S + 16
LAST_CUTS = (0, 512, 768, S)


def tile_list_shoe_patch_features_kernel(
    tc, tab_words, tab_scales, offs, pos1, pos2, pos3, w1, gain, w2_words, w2_scales, w3, out
):
    nc = tc.nc
    with ExitStack() as ctx:
        held = ctx.enter_context(tc.tile_pool(name="held", bufs=1))
        big = ctx.enter_context(tc.tile_pool(name="big", bufs=3))
        raws = ctx.enter_context(tc.tile_pool(name="raws", bufs=5))
        three = ctx.enter_context(tc.tile_pool(name="three", bufs=3))
        psum = ctx.enter_context(tc.psum_pool(name="psum", bufs=4))

        ys = [held.tile([P, Y_WIDTH], F32, name="y%d" % i) for i in range(3)]
        nc.gpsimd.memset(ys[0][:, M:S], 0.0)
        nc.scalar.activation(ys[0][:, S:], ys[0][:, M : M + Y_WIDTH - S], ACT.Silu)

        idx = held.tile([P, S // 16], U16, name="idx")
        p1 = held.tile([P, M // 16], U16, name="p1")
        p2 = held.tile([P, M // 16], U16, name="p2")
        p3 = held.tile([P, S // 16], U16, name="p3")
        nc.sync.dma_start(idx[:], offs)

        tab_s = held.tile([P, T], U8, name="tab_s", align_bytes=64)
        nc.vector.memset(tab_s[:].bitcast(I32), 0)
        w2s_raw = held.tile([P, 2, H], U8, name="w2s_raw", align_bytes=64)
        nc.gpsimd.memset(w2s_raw[:].bitcast(I32), 0)
        gains = held.tile([P, 2, PACK], F32, name="gains")

        v_words = [held.tile([P, S], U32, name="v_words%d" % g, align_bytes=64) for g in range(3)]
        v_scales = held.tile([P, S], U8, name="v_scales", align_bytes=64)

        def load_table(g, pieces=1):
            words = big.tile([P, T], U32, name="big", align_bytes=64)
            rows = tab_words[g].rearrange("p t i -> p (t i)").bitcast(I32)
            width = T // pieces
            for c0 in range(0, T, width):
                nc.sync.dma_start(words[:, c0 : c0 + width].bitcast(I32), rows[:, c0 : c0 + width])
            return words

        def gather_table(g, words):
            nc.vector.tensor_copy(v_words[g][:], words[:].indirect(idx[:]))

        def load_w1(g, b, pieces=1):
            raw = raws.tile([P, PACK, K_PASS], F32, name="raw")
            rows = w1[K_PASS * g : K_PASS * (g + 1), K_PASS * b : K_PASS * (b + 1)]
            rows = rows.rearrange("(p i) c -> p i c", i=PACK)
            depth = PACK // pieces
            for i0 in range(0, PACK, depth):
                nc.sync.dma_start(raw[:, i0 : i0 + depth, :], rows[:, i0 : i0 + depth, :])
            return raw[:]

        def load_w3(g):
            raw = big.tile([P, PACK, H], F32, name="big", align_bytes=64)
            nc.sync.dma_start(raw[:], w3[K_PASS * g : K_PASS * (g + 1), :].rearrange("(p i) c -> p i c", i=PACK))
            return raw

        def new_woven():
            return three.tile([P, PACK * K_PASS], BF16, name="woven", align_bytes=64)[:]

        def weave(copy, woven, raw, t0=0, slots=PACK):
            dealt = raw.rearrange("p i (m t) -> p m t i", t=PACK)[:, :, t0 : t0 + slots, :]
            copy(woven.rearrange("p (t m i) -> p m t i", t=slots, i=PACK), dealt)
            return woven

        def quantize(name, *parts):
            codes = held.tile([P, K_PASS], U32, name=name + "_codes", align_bytes=64)
            scales = held.tile([P, K_PASS], U8, name=name + "_scales", align_bytes=64)
            width = K_PASS // len(parts)
            for i, part in enumerate(parts):
                cols = slice(width * i, width * (i + 1))
                nc.vector.quantize_mx(out=codes[:, cols].bitcast(FP8X4), scales=scales[:, cols], in_=part)
            return codes, scales

        tab0 = load_table(0, pieces=4)
        raw00 = load_w1(0, 0, pieces=2)
        w2_raw = three.tile([P, 2, 2 * H], U8, name="woven", align_bytes=64)
        nc.sync.dma_start(w2_raw[:].bitcast(I32), w2_words.rearrange("g p c -> p g c").bitcast(I32))
        for q in range(4):
            nc.sync.dma_start(
                tab_s[32 * q : 32 * q + 12, :].bitcast(I32), tab_scales[:, 4 * q : 4 * q + 4, :].bitcast(I32)
            )
        tab1 = load_table(1)
        for q in range(4):
            nc.sync.dma_start(
                w2s_raw[32 * q : 32 * q + 4, :, :].bitcast(I32),
                w2_scales[:, 4 * q : 4 * q + 4, :].rearrange("g r c -> r g c").bitcast(I32),
            )
        raw10 = load_w1(1, 0)
        tab2 = load_table(2)
        raw20 = load_w1(2, 0)

        w2_codes = held.tile([P, 2, 2 * H], U8, name="w2_codes", align_bytes=64)
        w2_dealt_scales = held.tile([P, 2, H], U8, name="w2_dealt_scales", align_bytes=64)

        def deal_w2():
            words_out = w2_codes[:].rearrange("p g c -> p (g c)").bitcast(U16)
            words_in = w2_raw[:].rearrange("p g c -> p (g c)").bitcast(U16)
            nc.vector.tensor_copy(
                words_out.rearrange("p (e t u v) -> p e u t v", e=4, t=PACK, v=8),
                words_in.rearrange("p (e u v t) -> p e u t v", e=4, t=PACK, v=8),
            )
            nc.vector.tensor_copy(
                w2_dealt_scales[:].rearrange("p g (b t u v) -> p (g b) u t v", b=2, t=PACK, v=16),
                w2s_raw[:].rearrange("p g (b u v t) -> p (g b) u t v", b=2, t=PACK, v=16),
            )

        w1q = {}
        gather_table(0, tab0)
        nc.vector.tensor_copy(v_scales[:], tab_s[:].indirect(idx[:]))
        w1q[0, 0] = quantize("w1_00", weave(nc.scalar.copy, new_woven(), raw00))
        gather_table(1, tab1)
        deal_w2()
        w1q[1, 0] = quantize("w1_10", weave(nc.scalar.copy, new_woven(), raw10))
        gather_table(2, tab2)
        woven = new_woven()
        first_two, last_two = woven[:, : 2 * K_PASS], woven[:, 2 * K_PASS :]
        weave(nc.vector.tensor_copy, first_two, raw20, t0=0, slots=2)
        weave(nc.scalar.copy, last_two, raw20, t0=2, slots=2)
        w1q[2, 0] = quantize("w1_20", first_two, last_two)

        raw1 = [load_w1(g, 1) for g in range(3)]
        nc.sync.dma_start(p1[:], pos1)
        nc.sync.dma_start(p2[:], pos2)
        nc.sync.dma_start(gains[:], gain.rearrange("(b p t) -> p b t", b=2, t=PACK))
        nc.sync.dma_start(p3[:], pos3)
        raw3 = [load_w3(g) for g in range(2)]
        for y in ys[1:]:
            nc.gpsimd.memset(y[:, M:], 0.0)

        hs = [held.tile([P, S], F32, name="h%d" % s, align_bytes=64) for s in range(SLOTS)]
        angles = [held.tile([P, S], F32, name="angle%d" % i, align_bytes=64) for i in range(3)]
        z_rows = held.tile([P, PACK, M], BF16, name="z_rows", align_bytes=64)
        z_bytes = z_rows[:].rearrange("p t m -> p (t m)")
        accs, a_copies, pairs, smallest, zq, w3q, w3_woven = {}, {}, {}, {}, {}, {}, {}
        halves = [slice(0, BANK), slice(BANK, S)]

        def new_a_tile():
            return three.tile([P, S], F32, name="a_copy", bufs=4)

        def first_product(s, passes=(0, 1, 2)):
            b, t = divmod(s, PACK)
            cols = slice(P * t, P * (t + 1))
            if passes[0] == 0:
                accs[s] = [psum.tile([P, BANK], F32, name="acc%d" % u) for u in range(2)]
            for acc, js in zip(accs[s], halves):
                for g in passes:
                    codes, scales = w1q[g, b]
                    nc.tensor.matmul_mx(
                        out=acc[:], lhsT=codes[:, cols].bitcast(FP8X4), lhsT_scale=scales[:, cols],
                        rhs=v_words[g][:, js].bitcast(FP8X4), rhs_scale=v_scales[4 * g : P, js],
                        start=(g == 0), stop=(g == 2),
                    )

        def count_turns(engine, turns, a):
            engine.tensor_scalar(turns.bitcast(I32), a, 1.0 / TWO_PI, 0.0, ALU.mult, ALU.add)

        def turns_of(s):
            angle = angles[s % 3]
            if s == 0:
                for acc, js in zip(accs[s], halves):
                    count_turns(nc.vector, angle[:, js], acc[:])
                return
            a_copies[s] = new_a_tile()
            for acc, js in zip(accs[s], halves):
                nc.scalar.copy(a_copies[s][:, js], acc[:])
            count_turns(nc.vector, angle[:, :TURNS_ON_VECTOR], accs[s][0][:, :TURNS_ON_VECTOR])
            count_turns(nc.gpsimd, angle[:, TURNS_ON_VECTOR:], a_copies[s][:, TURNS_ON_VECTOR:])

        def reduce_angle(s):
            angle = angles[s % 3]
            for acc, js in zip(accs[s], halves):
                nc.vector.scalar_tensor_tensor(
                    angle[:, js], angle[:, js].bitcast(I32), -TWO_PI, acc[:], ALU.mult, ALU.add
                )

        def cosine(s):
            for js in halves if s == 0 else [slice(0, S)]:
                part = angles[s % 3][:, js]
                folded = angles[2][:] if s == LAST else part
                nc.scalar.activation(folded, part, ACT.Abs)
                nc.scalar.activation(part, folded, ACT.Sin, bias=math.pi / 2, scale=-1.0)

        def features(s):
            for u, js in enumerate(halves):
                if s == 0:
                    nc.vector.tensor_tensor(hs[s][:, js], accs[s][u][:], angles[0][:, js], ALU.mult)
                else:
                    nc.gpsimd.tensor_tensor(hs[s][:, js], a_copies[s][:, js], angles[s % 3][:, js], ALU.mult)

        def pick_pairs(s):
            pairs[s] = hs[s + 2] if s + 2 < SLOTS else new_a_tile()
            nc.vector.tensor_copy(pairs[s][:, :M], hs[s][:].indirect(p1[:]))
            nc.vector.tensor_copy(pairs[s][:, M:], hs[s][:].indirect(p2[:]))

        def new_row():
            return three.tile([P, M], F32, name="row")[:]

        def smaller(s):
            smallest[s] = new_row()
            nc.vector.tensor_tensor(smallest[s], pairs[s][:, :M], pairs[s][:, M:], ALU.min)

        def apply_gain(s):
            b, t = divmod(s, PACK)
            if s == LAST:
                nc.vector.tensor_scalar(z_rows[:, t, :], smallest[s], gains[:, b, t : t + 1], None, ALU.mult)
            else:
                nc.scalar.activation(z_rows[:, t, :], smallest[s], ACT.Copy, scale=gains[:, b, t : t + 1])

        def quantize_z(b, copy):
            z_woven = new_woven()
            copy(
                z_woven.rearrange("p (c v t) -> p c t v", v=4, t=PACK),
                z_rows[:].rearrange("p t (c v) -> p c t v", v=4),
            )
            zq[b] = quantize("z%d" % b, z_woven)

        w3_homes = {
            (0, 0): angles[2][:].bitcast(BF16),
            (1, 0): angles[0][:].bitcast(BF16),
            (0, 1): angles[1][:].bitcast(BF16),
            (1, 1): z_bytes,
        }

        def weave_w3(g, b):
            w3_woven[g, b] = weave(nc.scalar.copy, w3_homes[g, b], raw3[g][:, :, K_PASS * b : K_PASS * (b + 1)])

        def quantize_w3(g, b):
            w3q[g, b] = quantize("w3_%d%d" % (g, b), w3_woven[g, b])

        first_product(0, (0, 1))
        first_product(1, (0, 1))
        first_product(0, (2,))
        first_product(1, (2,))
        turns_of(0)
        reduce_angle(0)
        w1q[0, 1] = quantize("w1_01", weave(nc.vector.tensor_copy, new_woven(), raw1[0]))
        turns_of(1)
        first_product(2)
        cosine(0)
        reduce_angle(1)
        first_product(3)
        cosine(1)
        parts = [home[:, :BANK].bitcast(BF16) for home in (angles[2], hs[0])]
        for i, part in enumerate(parts):
            weave(nc.vector.tensor_copy, part, raw1[1], t0=2 * i, slots=2)
        w1q[1, 1] = quantize("w1_11", *parts)
        turns_of(2)
        features(0)
        turns_of(3)
        w1q[2, 1] = quantize("w1_21", weave(nc.scalar.copy, new_woven(), raw1[2]))

        w3_steps = {LAST - 1: [(0, 0), (1, 0)], LAST: [(0, 1)]}
        for s in range(SLOTS):
            if s >= 1:
                smaller(s - 1)
            if s + 1 < SLOTS:
                features(s + 1)
            if s + 2 < SLOTS:
                reduce_angle(s + 2)
                cosine(s + 2)
            if s + 4 < SLOTS:
                first_product(s + 4)
                turns_of(s + 4)
            if s >= 1:
                apply_gain(s - 1)
            for piece in w3_steps.get(s, []):
                weave_w3(*piece)
            pick_pairs(s)
            if s == PACK:
                quantize_z(0, nc.scalar.copy)
            for piece in w3_steps.get(s, []):
                quantize_w3(*piece)
        smaller(LAST)
        apply_gain(LAST)
        quantize_z(1, nc.vector.tensor_copy)

        factors = {}

        def second_products(s):
            b, t = divmod(s, PACK)
            cols = slice(P * t, P * (t + 1))
            c0 = K_PASS * b + P * t
            acc_w2 = psum.tile([P, M], F32, name="acc0")
            acc_w3 = psum.tile([P, M], F32, name="acc1")
            for g in range(2):
                nc.tensor.matmul_mx(
                    out=acc_w2[:], lhsT=w2_codes[:, g, 2 * c0 : 2 * (c0 + P)].bitcast(FP4X4),
                    lhsT_scale=w2_dealt_scales[:, g, c0 : c0 + P],
                    rhs=zq[g][0][:].bitcast(FP8X4), rhs_scale=zq[g][1][:], start=(g == 0), stop=(g == 1),
                )
            for g in range(2):
                codes, scales = w3q[g, b]
                nc.tensor.matmul_mx(
                    out=acc_w3[:], lhsT=codes[:, cols].bitcast(FP8X4), lhsT_scale=scales[:, cols],
                    rhs=zq[g][0][:].bitcast(FP8X4), rhs_scale=zq[g][1][:], start=(g == 0), stop=(g == 1),
                )
            factor = z_bytes.bitcast(F32)[:, :M] if s == 0 else new_row()
            nc.scalar.copy(factor, acc_w2[:])
            factors[s] = (factor, acc_w3)

        def multiply(s):
            factor, acc_w3 = factors[s]
            nc.vector.tensor_tensor(ys[s % 3][:, :M], acc_w3[:], factor, ALU.mult)

        def finish(s):
            b, t = divmod(s, PACK)
            cuts = LAST_CUTS if s == LAST else (0, S)
            rows = out[K_PASS * b : K_PASS * (b + 1), :].rearrange("(p t) j -> p t j", t=PACK)
            for j0, j1 in zip(cuts, cuts[1:]):
                total = raws.tile([P, j1 - j0], F32, name="raw")
                nc.vector.tensor_tensor(
                    total[:], ys[s % 3][:].indirect(p3[:, j0 // 16 : j1 // 16]), hs[s][:, j0:j1], ALU.add
                )
                nc.scalar.activation(total[:], total[:], ACT.Tanh)
                nc.sync.dma_start(rows[:, t, j0:j1], total[:])

        second_products(0)
        second_products(1)
        multiply(0)
        for s in range(SLOTS):
            if s + 2 < SLOTS:
                second_products(s + 2)
            if s + 1 < SLOTS:
                multiply(s + 1)
            if s == 0:
                weave_w3(1, 1)
            finish(s)
            if s == 0:
                quantize_w3(1, 1)
